import numpy as np
import ml_dtypes


def mxq(x, axis, fmt="e4m3"):
    dtype, down = {"e4m3": (ml_dtypes.float8_e4m3fn, 7), "e5m2": (ml_dtypes.float8_e5m2, 14)}[fmt]
    v = np.moveaxis(np.asarray(x, np.float32).astype(ml_dtypes.bfloat16).astype(np.float64), axis, -1)
    blocks = v.reshape(v.shape[:-1] + (-1, 32))
    amax = np.abs(blocks).max(-1, keepdims=True)
    byte = np.maximum(np.where(amax > 0, np.frexp(amax)[1] - 1 + 127, 0) - down, 1)
    scale = np.exp2(byte - 127.0)
    codes = (blocks / scale).astype(np.float32).astype(dtype).astype(np.float64)
    return np.moveaxis((codes * scale).reshape(v.shape), -1, axis)


WIDE = False


def mx_kscale(k):
    if not WIDE:
        return np.ones(k)
    levels = np.array([10, -10, 5, -5, 0])
    if k % 512:
        return np.exp2(np.random.permutation(np.resize(levels, k // 32))).repeat(32)
    a = np.empty((k // 512, 16))
    for p in range(k // 512):
        a[p, :8] = np.random.permutation(np.resize(levels, 8))
        for g in range(8):
            far = levels[np.abs(levels - a[p, g]) >= 10]
            a[p, g + 8] = far[np.random.randint(len(far))]
    return np.exp2(a.ravel()).repeat(32)


def f64(x):
    return np.asarray(x).astype(np.float64)


def striped8(idx):
    return np.concatenate([v.reshape(-1, 16).T for v in idx]).astype(np.uint16)


def unstriped8(offs):
    return np.stack([offs[16 * g:16 * g + 16].T.reshape(-1) for g in range(8)]).astype(np.int64)


E2M1 = np.array([0.0, 0.5, 1.0, 1.5, 2.0, 3.0, 4.0, 6.0, -0.0, -0.5, -1.0, -1.5, -2.0, -3.0, -4.0, -6.0])


def pack_weight(w, fmt):
    k, n = w.shape
    w = f64(np.asarray(w, np.float32).astype(ml_dtypes.bfloat16)).reshape(k // 32, 32, n)
    amax = np.abs(w).max(1)
    if fmt == "e4m3":
        byte = np.frexp(amax)[1] - 1 + 127 - 7
    else:
        mant, ex = np.frexp(amax / 6.0)
        byte = np.where(mant > 0.5, ex, ex - 1) + 127
    byte = np.clip(np.where(amax > 0, byte, 1), 1, 254)
    scaled = (w * np.exp2(127.0 - byte)[:, None, :]).reshape(k, n).astype(np.float32)
    by_word = np.ascontiguousarray(scaled.reshape(k // 512, 128, 4, n).transpose(0, 1, 3, 2))
    if fmt == "e4m3":
        words = by_word.astype(ml_dtypes.float8_e4m3fn).view(np.uint8)
    else:
        c = by_word.astype(ml_dtypes.float4_e2m1fn).view(np.uint8) & 0xF
        words = (c[..., 0::2] | (c[..., 1::2] << 4)).reshape(k // 512, 128, 2 * n)
    return np.ascontiguousarray(words), np.ascontiguousarray(byte.astype(np.uint8).reshape(k // 512, 16, n))


def unpack_weight(words, scales, fmt):
    g, _, n = scales.shape
    words = np.ascontiguousarray(words).reshape(g, 128, n, -1)
    if fmt == "e4m3":
        vals = words.view(ml_dtypes.float8_e4m3fn).astype(np.float64)
    else:
        nib = np.empty((g, 128, n, 4), np.uint8)
        nib[..., 0::2] = words & 0xF
        nib[..., 1::2] = words >> 4
        vals = E2M1[nib]
    vals = vals * np.repeat(np.exp2(scales.astype(np.float64) - 127.0), 8, axis=1)[..., None]
    return vals.transpose(0, 1, 3, 2).reshape(g * 512, n)


def silu(v):
    return v / (1.0 + np.exp(-np.maximum(v, -700.0)))


K, M, T, S = 1024, 128, 2048, 1024


def setup_inputs():
    n = np.random.standard_normal
    s = mx_kscale(K)[:, None]
    p_w = pack_weight(n((K, M)) / np.sqrt(K) / s, "e4m3")
    return {
        "xT": (n((K, T)) * s).astype(np.float32),
        "w_words": p_w[0],
        "w_scales": p_w[1],
        "wgt": np.repeat(np.random.uniform(0.5, 2.0, (8, S)), 16, axis=0).astype(np.float32),
        "b": (0.3 * n(128)).astype(np.float32),
        "offs": striped8(np.stack([np.random.permutation(T)[:S] for _ in range(8)])),
    }


def reference(xT, w_words, w_scales, wgt, b, offs):
    idx = unstriped8(offs)
    group = np.arange(K) % 512 // 64
    xg = f64(wgt)[np.arange(K) // 4 % 128] * f64(xT)[np.arange(K)[:, None], idx[group]]
    xT_ = mxq(xg, 0, "e4m3")
    w_ = unpack_weight(w_words, w_scales, "e4m3")
    y = xT_.T @ w_
    return silu(y + f64(b)[None, :])

@@ -1,0 +1,187 @@
+from contextlib import ExitStack
+
+import concourse.mybir as mybir
+from concourse.masks import make_identity
+
+F32 = mybir.dt.float32
+BF16 = mybir.dt.bfloat16
+I32 = mybir.dt.int32
+U32 = mybir.dt.uint32
+U16 = mybir.dt.uint16
+U8 = mybir.dt.uint8
+FP8X4 = mybir.dt.float8_e4m3fn_x4
+MULT = mybir.AluOpType.mult
+ADD = mybir.AluOpType.add
+SILU = mybir.ActivationFunctionType.Silu
+
+K, M, T, S = 1024, 128, 2048, 1024
+FLOPS = 2 * K * M * S
+
+P = 128
+PACK = 4
+PASSES = K // (P * PACK)
+PLANES = PASSES * PACK
+LANES = 16
+
+HALVES = [(0, 512), (512, 512)]
+
+TURNED_SLICES = [(0, 256), (256, 256)]
+DIRECT_SLICES = [(512, 256), (768, 128), (896, 128)]
+LAST_SLICE = DIRECT_SLICES[-1]
+
+PLANE_6_PIECES = [(512, 256), (768, 256)]
+
+
+def tile_list_heads_tm_silu_kernel(tc, xT, w_words, w_scales, wgt, b, offs, out):
+    nc = tc.nc
+    with ExitStack() as ctx:
+        keep = ctx.enter_context(tc.tile_pool(name="keep", bufs=1))
+        psum = ctx.enter_context(tc.psum_pool(name="psum", bufs=1))
+
+        offsets = keep.tile([P, S // LANES], U16, name="offsets")
+        nc.sync.dma_start(offsets[:], offs)
+
+        plane_rows = xT.rearrange("(a p i) t -> a i p t", p=P, i=PACK)
+        planes = [keep.tile([P, T], F32, name=f"plane{u}") for u in range(PLANES)]
+        token_weights = keep.tile([P, S], F32, name="token_weights")
+        w_codes = keep.tile([P, PASSES, M], U32, name="w_codes", align_bytes=64)
+        w_scale_rows = keep.tile([P, PASSES, M], U8, name="w_scale_rows", align_bytes=64)
+        b_column = keep.tile([P, 1], F32, name="b_column")
+
+        def load_plane(u):
+            nc.sync.dma_start(planes[u][:], plane_rows[u // PACK, u % PACK])
+
+        load_plane(0)
+        for j0, n in HALVES:
+            nc.sync.dma_start(token_weights[:, j0 : j0 + n], wgt[:, j0 : j0 + n])
+        for u in range(1, 6):
+            load_plane(u)
+
+        warm_up = keep.tile([P, 1], F32, name="warm_up")
+        nc.vector.memset(warm_up[:], 0.0)
+        nc.scalar.activation(warm_up[:], warm_up[:], SILU)
+        nc.vector.memset(w_scale_rows[:].rearrange("p a n -> p (a n)").bitcast(I32), 0)
+        identity = keep.tile([P, P], F32, name="identity")
+        make_identity(nc, identity[:])
+
+        nc.sync.dma_start(w_codes[:].bitcast(I32), w_words.rearrange("a p n i -> p a (n i)").bitcast(I32))
+        scale_source = w_scales.bitcast(I32).rearrange("a q n -> q a n")
+        for quadrant in range(4):
+            nc.sync.dma_start(
+                w_scale_rows[32 * quadrant : 32 * quadrant + 4].bitcast(I32),
+                scale_source[4 * quadrant : 4 * quadrant + 4],
+            )
+        nc.sync.dma_start(b_column[:], b.rearrange("(p o) -> p o", o=1))
+        load_plane(6)
+        load_plane(7)
+
+        grouped = [keep.tile([P, S, PACK], BF16, name=f"grouped{a}", align_bytes=64) for a in range(PASSES)]
+        codes = [keep.tile([P, S], U32, name=f"codes{a}", align_bytes=64) for a in range(PASSES)]
+        scales = [keep.tile([P, S], U8, name=f"scales{a}", align_bytes=64) for a in range(PASSES)]
+
+        def picked_tiles(u, count):
+            return [keep.tile([P, count, n], F32, name=f"picked{u}_{j0}") for j0, n in HALVES]
+
+        def gather(picked, u, j0, n):
+            nc.vector.tensor_tensor(
+                picked,
+                planes[u][:].indirect(offsets[:, j0 // LANES : (j0 + n) // LANES]),
+                token_weights[:, j0 : j0 + n],
+                MULT,
+            )
+
+        def interleave(copy, picked, u, j0, n):
+            i0 = u % PACK
+            copy(
+                grouped[u // PACK][:, j0 : j0 + n, i0 : i0 + picked.shape[1]],
+                picked.rearrange("p i j -> p j i"),
+            )
+
+        def quantise(a, j0, n):
+            nc.vector.quantize_mx(
+                out=codes[a][:, j0 : j0 + n].bitcast(FP8X4),
+                scales=scales[a][:, j0 : j0 + n],
+                in_=grouped[a][:, j0 : j0 + n, :].rearrange("p j i -> p (j i)"),
+            )
+
+        def project_turned(j0, n):
+            acc = psum.tile([P, n], F32, name=f"acc{j0}")
+            for a in range(PASSES):
+                nc.tensor.matmul_mx(
+                    out=acc[:],
+                    lhsT=w_codes[:, a, :].bitcast(FP8X4),
+                    lhsT_scale=w_scale_rows[:, a, :],
+                    rhs=codes[a][:, j0 : j0 + n].bitcast(FP8X4),
+                    rhs_scale=scales[a][:, j0 : j0 + n],
+                    start=(a == 0),
+                    stop=(a == PASSES - 1),
+                )
+            columns = keep.tile([P, n], F32, name=f"columns{j0}")
+            nc.scalar.activation(columns[:], acc[:], SILU, bias=b_column[:])
+            turned = psum.tile([P, n // P, P], F32, name=f"turned{j0}")
+            for c in range(n // P):
+                nc.tensor.transpose(turned[:, c, :], columns[:, c * P : (c + 1) * P], identity[:])
+            rows = keep.tile([P, n // P, P], F32, name=f"rows{j0}")
+            nc.scalar.copy(rows[:], turned[:])
+            nc.sync.dma_start(out[j0 : j0 + n, :].rearrange("(c p) n -> p c n", p=P), rows[:])
+
+        def project_direct(store, j0, n):
+            acc = psum.tile([P, n // P, P], F32, name=f"acc{j0}")
+            for c in range(n // P):
+                tokens = slice(j0 + c * P, j0 + (c + 1) * P)
+                for a in range(PASSES):
+                    nc.tensor.matmul_mx(
+                        out=acc[:, c, :],
+                        lhsT=codes[a][:, tokens].bitcast(FP8X4),
+                        lhsT_scale=scales[a][:, tokens],
+                        rhs=w_codes[:, a, :].bitcast(FP8X4),
+                        rhs_scale=w_scale_rows[:, a, :],
+                        start=(a == 0),
+                        stop=(a == PASSES - 1),
+                    )
+            biased = keep.tile([P, n // P, P], F32, name=f"biased{j0}")
+            nc.vector.tensor_tensor(biased[:], acc[:], b_rows[:].unsqueeze(1).to_broadcast([P, n // P, P]), ADD)
+            rows = keep.tile([P, n // P, P], F32, name=f"rows{j0}")
+            nc.scalar.activation(rows[:], biased[:], SILU)
+            store(out[j0 : j0 + n, :].rearrange("(c p) n -> p c n", p=P), rows[:])
+
+        b_turned = psum.tile([P, P], F32, name="b_turned")
+        nc.tensor.transpose(b_turned[:], b_column[:].to_broadcast([P, P]), identity[:])
+        b_rows = keep.tile([P, P], F32, name="b_rows")
+        nc.scalar.copy(b_rows[:], b_turned[:])
+
+        picked = picked_tiles(0, 4)
+        for u in range(4):
+            for h, (j0, n) in enumerate(HALVES):
+                gather(picked[h][:, u, :], u, j0, n)
+        for h, (j0, n) in enumerate(HALVES):
+            interleave(nc.scalar.copy, picked[h][:], 0, j0, n)
+
+        picked = picked_tiles(4, 2)
+        for u in (4, 5):
+            for h, (j0, n) in enumerate(HALVES):
+                gather(picked[h][:, u - 4, :], u, j0, n)
+        for h, (j0, n) in enumerate(HALVES):
+            interleave(nc.scalar.copy, picked[h][:], 4, j0, n)
+
+        front, back = picked_tiles(6, 2)
+        gather(front[:, 0, :], 6, 0, 512)
+        for j0, n in TURNED_SLICES:
+            gather(front[:, 1, j0 : j0 + n], 7, j0, n)
+            interleave(nc.scalar.copy, front[:, :, j0 : j0 + n], 6, j0, n)
+            if j0 == 0:
+                for first, tokens in HALVES:
+                    quantise(0, first, tokens)
+            quantise(1, j0, n)
+            project_turned(j0, n)
+
+        for j0, n in PLANE_6_PIECES:
+            gather(back[:, 0, j0 - 512 : j0 - 512 + n], 6, j0, n)
+        for j0, n in DIRECT_SLICES:
+            is_last = (j0, n) == LAST_SLICE
+            gather(back[:, 1, j0 - 512 : j0 - 512 + n], 7, j0, n)
+            copy = nc.vector.tensor_copy if is_last else nc.scalar.copy
+            store = nc.scalar.dma_start if is_last else nc.sync.dma_start
+            interleave(copy, back[:, :, j0 - 512 : j0 - 512 + n], 6, j0, n)
+            quantise(1, j0, n)
+            project_direct(store, j0, n)

@@ -23,13 +23,13 @@ PASSES = K // (P * PACK)
 PLANES = PASSES * PACK
 LANES = 16
 
+GROUPS = P // LANES
+BLOCKS = S // P
+
 HALVES = [(0, 512), (512, 512)]
-
-TURNED_SLICES = [(0, 256), (256, 256)]
-DIRECT_SLICES = [(512, 256), (768, 128), (896, 128)]
-LAST_SLICE = DIRECT_SLICES[-1]
-
-PLANE_6_PIECES = [(512, 256), (768, 256)]
+QUARTERS = [(j0, 256) for j0 in range(0, S, 256)]
+WEIGHT_PIECES = [(0, 128), (128, 128), (256, 256), (512, 256), (768, 256)]
+PIECES = {0: [(0, 128), (128, 384), (512, 512)], 5: HALVES}
 
 
 def tile_list_heads_tm_silu_kernel(tc, xT, w_words, w_scales, wgt, b, offs, out):
@@ -38,31 +38,34 @@ def tile_list_heads_tm_silu_kernel(tc, xT, w_words, w_scales, wgt, b, offs, out)
         keep = ctx.enter_context(tc.tile_pool(name="keep", bufs=1))
         psum = ctx.enter_context(tc.psum_pool(name="psum", bufs=1))
 
-        offsets = keep.tile([P, S // LANES], U16, name="offsets")
-        nc.sync.dma_start(offsets[:], offs)
+        def bank(index, shape, name):
+            return psum.tile(shape, F32, name=name, tag=f"bank{index}")
+
+        small_rows = keep.tile([P, P], F32, name="small_rows")
+        nc.vector.memset(small_rows[64:95, :], 0.0)
+        nc.vector.memset(small_rows[96:128, :], 0.0)
+        nc.sync.dma_start(
+            small_rows[0:64, :], wgt.rearrange("(g l) (h j) -> l h g j", l=LANES, j=P)[0]
+        )
+        nc.sync.dma_start(small_rows[95:96, :], b.rearrange("(o n) -> o n", o=1))
 
         plane_rows = xT.rearrange("(a p i) t -> a i p t", p=P, i=PACK)
-        planes = [keep.tile([P, T], F32, name=f"plane{u}") for u in range(PLANES)]
-        token_weights = keep.tile([P, S], F32, name="token_weights")
+        planes = [keep.tile([P, T], F32, name=f"plane{u}", tag=f"plane{u}", align_bytes=64) for u in range(PLANES)]
+        offsets = keep.tile([P, S // LANES], U16, name="offsets")
         w_codes = keep.tile([P, PASSES, M], U32, name="w_codes", align_bytes=64)
         w_scale_rows = keep.tile([P, PASSES, M], U8, name="w_scale_rows", align_bytes=64)
-        b_column = keep.tile([P, 1], F32, name="b_column")
 
-        def load_plane(u):
+        for u in range(PLANES):
             nc.sync.dma_start(planes[u][:], plane_rows[u // PACK, u % PACK])
+            if u == 0:
+                nc.sync.dma_start(offsets[:], offs)
 
-        load_plane(0)
-        for j0, n in HALVES:
-            nc.sync.dma_start(token_weights[:, j0 : j0 + n], wgt[:, j0 : j0 + n])
-        for u in range(1, 6):
-            load_plane(u)
-
+        identity = keep.tile([P, P], F32, name="identity")
+        make_identity(nc, identity[:])
         warm_up = keep.tile([P, 1], F32, name="warm_up")
         nc.vector.memset(warm_up[:], 0.0)
         nc.scalar.activation(warm_up[:], warm_up[:], SILU)
         nc.vector.memset(w_scale_rows[:].rearrange("p a n -> p (a n)").bitcast(I32), 0)
-        identity = keep.tile([P, P], F32, name="identity")
-        make_identity(nc, identity[:])
 
         nc.sync.dma_start(w_codes[:].bitcast(I32), w_words.rearrange("a p n i -> p a (n i)").bitcast(I32))
         scale_source = w_scales.bitcast(I32).rearrange("a q n -> q a n")
@@ -71,22 +74,43 @@ def tile_list_heads_tm_silu_kernel(tc, xT, w_words, w_scales, wgt, b, offs, out)
                 w_scale_rows[32 * quadrant : 32 * quadrant + 4].bitcast(I32),
                 scale_source[4 * quadrant : 4 * quadrant + 4],
             )
-        nc.sync.dma_start(b_column[:], b.rearrange("(p o) -> p o", o=1))
-        load_plane(6)
-        load_plane(7)
+
+        small_columns = bank(7, [P, P], "small_columns")
+        nc.tensor.transpose(small_columns[:], small_rows[:], identity[:])
+        token_weights = keep.tile([P, S], F32, name="token_weights")
+        late_weights = keep.tile([P, 256], F32, name="late_weights", tag="late", align_bytes=64)
+        for q, (j0, n) in enumerate(WEIGHT_PIECES):
+            columns = n // P * GROUPS
+            spread = keep.tile([P, columns, LANES], F32, name=f"spread{q}")
+            first = j0 // P * GROUPS
+            nc.vector.tensor_copy(
+                spread[:], small_columns[:, first : first + columns].unsqueeze(2).to_broadcast([P, columns, LANES])
+            )
+            turned_back = bank(q, [P, n], f"turned_back{q}")
+            for c in range(n // P):
+                nc.tensor.transpose(
+                    turned_back[:, c * P : (c + 1) * P],
+                    spread[:].rearrange("p a l -> p (a l)")[:, c * P : (c + 1) * P],
+                    identity[:],
+                )
+            nc.scalar.copy(token_weights[:, j0 : j0 + n], turned_back[:])
+        nc.scalar.copy(late_weights[:], token_weights[:, 0:256])
+        b_column = keep.tile([P, 1], F32, name="b_column")
+        nc.vector.tensor_copy(b_column[:], small_columns[:, 95:96])
+        b_turned = bank(6, [P, P], "b_turned")
+        nc.tensor.transpose(b_turned[:], b_column[:].to_broadcast([P, P]), identity[:])
+        b_rows = keep.tile([P, P], F32, name="b_rows")
+        nc.scalar.copy(b_rows[:], b_turned[:])
 
         grouped = [keep.tile([P, S, PACK], BF16, name=f"grouped{a}", align_bytes=64) for a in range(PASSES)]
-        codes = [keep.tile([P, S], U32, name=f"codes{a}", align_bytes=64) for a in range(PASSES)]
+        codes = {}
         scales = [keep.tile([P, S], U8, name=f"scales{a}", align_bytes=64) for a in range(PASSES)]
 
-        def picked_tiles(u, count):
-            return [keep.tile([P, count, n], F32, name=f"picked{u}_{j0}") for j0, n in HALVES]
-
-        def gather(picked, u, j0, n):
+        def gather(picked, u, j0, n, weights=None):
             nc.vector.tensor_tensor(
                 picked,
                 planes[u][:].indirect(offsets[:, j0 // LANES : (j0 + n) // LANES]),
-                token_weights[:, j0 : j0 + n],
+                token_weights[:, j0 : j0 + n] if weights is None else weights,
                 MULT,
             )
 
@@ -97,43 +121,47 @@ def tile_list_heads_tm_silu_kernel(tc, xT, w_words, w_scales, wgt, b, offs, out)
                 picked.rearrange("p i j -> p j i"),
             )
 
+        def codes_of(a, j0, n):
+            half = j0 // 512
+            return codes[a, half][:, j0 - 512 * half : j0 - 512 * half + n].bitcast(FP8X4)
+
         def quantise(a, j0, n):
             nc.vector.quantize_mx(
-                out=codes[a][:, j0 : j0 + n].bitcast(FP8X4),
+                out=codes_of(a, j0, n),
                 scales=scales[a][:, j0 : j0 + n],
                 in_=grouped[a][:, j0 : j0 + n, :].rearrange("p j i -> p (j i)"),
             )
 
-        def project_turned(j0, n):
-            acc = psum.tile([P, n], F32, name=f"acc{j0}")
+        def project_turned(first_bank, j0, n):
+            acc = bank(first_bank, [P, n], f"acc{j0}")
             for a in range(PASSES):
                 nc.tensor.matmul_mx(
                     out=acc[:],
                     lhsT=w_codes[:, a, :].bitcast(FP8X4),
                     lhsT_scale=w_scale_rows[:, a, :],
-                    rhs=codes[a][:, j0 : j0 + n].bitcast(FP8X4),
+                    rhs=codes_of(a, j0, n),
                     rhs_scale=scales[a][:, j0 : j0 + n],
                     start=(a == 0),
                     stop=(a == PASSES - 1),
                 )
             columns = keep.tile([P, n], F32, name=f"columns{j0}")
             nc.scalar.activation(columns[:], acc[:], SILU, bias=b_column[:])
-            turned = psum.tile([P, n // P, P], F32, name=f"turned{j0}")
+            turned = bank(first_bank + 1, [P, n // P, P], f"turned{j0}")
             for c in range(n // P):
                 nc.tensor.transpose(turned[:, c, :], columns[:, c * P : (c + 1) * P], identity[:])
             rows = keep.tile([P, n // P, P], F32, name=f"rows{j0}")
             nc.scalar.copy(rows[:], turned[:])
             nc.sync.dma_start(out[j0 : j0 + n, :].rearrange("(c p) n -> p c n", p=P), rows[:])
 
-        def project_direct(store, j0, n):
-            acc = psum.tile([P, n // P, P], F32, name=f"acc{j0}")
+        def project_direct(store, index, j0, n):
+            acc = bank(index, [P, n // P, P], f"acc{j0}")
             for c in range(n // P):
-                tokens = slice(j0 + c * P, j0 + (c + 1) * P)
+                first = j0 + c * P
                 for a in range(PASSES):
                     nc.tensor.matmul_mx(
                         out=acc[:, c, :],
-                        lhsT=codes[a][:, tokens].bitcast(FP8X4),
-                        lhsT_scale=scales[a][:, tokens],
+                        lhsT=codes_of(a, first, P),
+                        lhsT_scale=scales[a][:, first : first + P],
                         rhs=w_codes[:, a, :].bitcast(FP8X4),
                         rhs_scale=w_scale_rows[:, a, :],
                         start=(a == 0),
@@ -145,43 +173,55 @@ def tile_list_heads_tm_silu_kernel(tc, xT, w_words, w_scales, wgt, b, offs, out)
             nc.scalar.activation(rows[:], biased[:], SILU)
             store(out[j0 : j0 + n, :].rearrange("(c p) n -> p c n", p=P), rows[:])
 
-        b_turned = psum.tile([P, P], F32, name="b_turned")
-        nc.tensor.transpose(b_turned[:], b_column[:].to_broadcast([P, P]), identity[:])
-        b_rows = keep.tile([P, P], F32, name="b_rows")
-        nc.scalar.copy(b_rows[:], b_turned[:])
+        for u0 in (0, 2, 4):
+            if u0 < 4:
+                picked = keep.tile([P, 2, S], F32, name=f"picked{u0}")
+                for u in (u0, u0 + 1):
+                    for j0, n in PIECES.get(u, [(0, S)]):
+                        gather(picked[:, u - u0, j0 : j0 + n], u, j0, n)
+                for j0, n in HALVES if u0 == 2 else [(0, S)]:
+                    interleave(nc.scalar.copy, picked[:, :, j0 : j0 + n], u0, j0, n)
+            else:
+                picked = keep.tile([P, 2, S], F32, name=f"picked{u0}")
+                gather(picked[:, 0, :], 4, 0, S)
+                for j0, n in HALVES:
+                    gather(picked[:, 1, j0 : j0 + n], 5, j0, n)
+                for j0, n in HALVES:
+                    interleave(nc.scalar.copy, picked[:, :, j0 : j0 + n], u0, j0, n)
 
-        picked = picked_tiles(0, 4)
-        for u in range(4):
-            for h, (j0, n) in enumerate(HALVES):
-                gather(picked[h][:, u, :], u, j0, n)
-        for h, (j0, n) in enumerate(HALVES):
-            interleave(nc.scalar.copy, picked[h][:], 0, j0, n)
+        codes[0, 0] = keep.tile([P, 512], U32, name="codes00", align_bytes=64)
+        quantise(0, 0, 512)
+        codes[1, 0] = keep.tile([P, 512], U32, name="codes10", align_bytes=64)
+        codes[1, 1] = keep.tile([P, 512], U32, name="codes11", align_bytes=64)
 
-        picked = picked_tiles(4, 2)
-        for u in (4, 5):
-            for h, (j0, n) in enumerate(HALVES):
-                gather(picked[h][:, u - 4, :], u, j0, n)
-        for h, (j0, n) in enumerate(HALVES):
-            interleave(nc.scalar.copy, picked[h][:], 4, j0, n)
+        def picked_pair(j0, n, slot):
+            return keep.tile([P, 2, n], F32, name=f"pair{j0}", tag=f"ring{slot}")
 
-        front, back = picked_tiles(6, 2)
-        gather(front[:, 0, :], 6, 0, 512)
-        for j0, n in TURNED_SLICES:
-            gather(front[:, 1, j0 : j0 + n], 7, j0, n)
-            interleave(nc.scalar.copy, front[:, :, j0 : j0 + n], 6, j0, n)
-            if j0 == 0:
-                for first, tokens in HALVES:
-                    quantise(0, first, tokens)
-            quantise(1, j0, n)
-            project_turned(j0, n)
+        front = [picked_pair(256 * q, 256, q) for q in range(2)]
+        for q in range(2):
+            gather(front[q][:, 0, :], 6, 256 * q, 256)
+        gather(front[0][:, 1, :], 7, 0, 256, late_weights[:])
+        gather(front[1][:, 1, :], 7, 256, 256)
+        codes[0, 1] = keep.tile([P, 512], U32, name="codes01", tag="late", align_bytes=64)
+        quantise(0, 512, 512)
+        for q in (0, 1):
+            interleave(nc.scalar.copy, front[q][:], 6, 256 * q, 256)
+            quantise(1, 256 * q, 256)
+            project_turned(2 * q, 256 * q, 256)
 
-        for j0, n in PLANE_6_PIECES:
-            gather(back[:, 0, j0 - 512 : j0 - 512 + n], 6, j0, n)
-        for j0, n in DIRECT_SLICES:
-            is_last = (j0, n) == LAST_SLICE
-            gather(back[:, 1, j0 - 512 : j0 - 512 + n], 7, j0, n)
-            copy = nc.vector.tensor_copy if is_last else nc.scalar.copy
-            store = nc.scalar.dma_start if is_last else nc.sync.dma_start
-            interleave(copy, back[:, :, j0 - 512 : j0 - 512 + n], 6, j0, n)
-            quantise(1, j0, n)
-            project_direct(store, j0, n)
+        third = picked_pair(512, 256, 0)
+        for u in (6, 7):
+            gather(third[:, u - 6, :], u, 512, 256)
+        interleave(nc.scalar.copy, third[:], 6, 512, 256)
+        quantise(1, 512, 256)
+        project_direct(nc.sync.dma_start, 4, 512, 256)
+
+        fourth = picked_pair(768, 256, 1)
+        gather(fourth[:, 0, :], 6, 768, 256)
+        for c in range(2):
+            gather(fourth[:, 1, c * P : (c + 1) * P], 7, 768 + c * P, P)
+        for c, (copy, store) in enumerate([(nc.scalar.copy, nc.sync.dma_start), (nc.vector.tensor_copy, nc.scalar.dma_start)]):
+            j0 = 768 + c * P
+            interleave(copy, fourth[:, :, c * P : (c + 1) * P], 6, j0, P)
+            quantise(1, j0, P)
+            project_direct(store, 6 + c, j0, P)

@@ -42,12 +42,10 @@ def tile_list_heads_tm_silu_kernel(tc, xT, w_words, w_scales, wgt, b, offs, out)
             return psum.tile(shape, F32, name=name, tag=f"bank{index}")
 
         small_rows = keep.tile([P, P], F32, name="small_rows")
-        nc.vector.memset(small_rows[64:95, :], 0.0)
-        nc.vector.memset(small_rows[96:128, :], 0.0)
+        nc.vector.memset(small_rows[64:128, :], 0.0)
         nc.sync.dma_start(
             small_rows[0:64, :], wgt.rearrange("(g l) (h j) -> l h g j", l=LANES, j=P)[0]
         )
-        nc.sync.dma_start(small_rows[95:96, :], b.rearrange("(o n) -> o n", o=1))
 
         plane_rows = xT.rearrange("(a p i) t -> a i p t", p=P, i=PACK)
         planes = [keep.tile([P, T], F32, name=f"plane{u}", tag=f"plane{u}", align_bytes=64) for u in range(PLANES)]
@@ -55,10 +53,13 @@ def tile_list_heads_tm_silu_kernel(tc, xT, w_words, w_scales, wgt, b, offs, out)
         w_codes = keep.tile([P, PASSES, M], U32, name="w_codes", align_bytes=64)
         w_scale_rows = keep.tile([P, PASSES, M], U8, name="w_scale_rows", align_bytes=64)
 
+        b_column = keep.tile([P, 1], F32, name="b_column")
         for u in range(PLANES):
             nc.sync.dma_start(planes[u][:], plane_rows[u // PACK, u % PACK])
             if u == 0:
                 nc.sync.dma_start(offsets[:], offs)
+            if u == 3:
+                nc.sync.dma_start(b_column[:], b.rearrange("(p o) -> p o", o=1))
 
         identity = keep.tile([P, P], F32, name="identity")
         make_identity(nc, identity[:])
@@ -95,13 +96,6 @@ def tile_list_heads_tm_silu_kernel(tc, xT, w_words, w_scales, wgt, b, offs, out)
                 )
             nc.scalar.copy(token_weights[:, j0 : j0 + n], turned_back[:])
         nc.scalar.copy(late_weights[:], token_weights[:, 0:256])
-        b_column = keep.tile([P, 1], F32, name="b_column")
-        nc.vector.tensor_copy(b_column[:], small_columns[:, 95:96])
-        b_turned = bank(6, [P, P], "b_turned")
-        nc.tensor.transpose(b_turned[:], b_column[:].to_broadcast([P, P]), identity[:])
-        b_rows = keep.tile([P, P], F32, name="b_rows")
-        nc.scalar.copy(b_rows[:], b_turned[:])
-
         grouped = [keep.tile([P, S, PACK], BF16, name=f"grouped{a}", align_bytes=64) for a in range(PASSES)]
         codes = {}
         scales = [keep.tile([P, S], U8, name=f"scales{a}", align_bytes=64) for a in range(PASSES)]
@@ -132,26 +126,35 @@ def tile_list_heads_tm_silu_kernel(tc, xT, w_words, w_scales, wgt, b, offs, out)
                 in_=grouped[a][:, j0 : j0 + n, :].rearrange("p j i -> p (j i)"),
             )
 
-        def project_turned(first_bank, j0, n):
+        def project_turned(first_bank, j0, pieces):
+            n = sum(pieces)
             acc = bank(first_bank, [P, n], f"acc{j0}")
-            for a in range(PASSES):
-                nc.tensor.matmul_mx(
-                    out=acc[:],
-                    lhsT=w_codes[:, a, :].bitcast(FP8X4),
-                    lhsT_scale=w_scale_rows[:, a, :],
-                    rhs=codes_of(a, j0, n),
-                    rhs_scale=scales[a][:, j0 : j0 + n],
-                    start=(a == 0),
-                    stop=(a == PASSES - 1),
-                )
+            first = j0
+            for width in pieces:
+                for a in range(PASSES):
+                    nc.tensor.matmul_mx(
+                        out=acc[:, first - j0 : first - j0 + width],
+                        lhsT=w_codes[:, a, :].bitcast(FP8X4),
+                        lhsT_scale=w_scale_rows[:, a, :],
+                        rhs=codes_of(a, first, width),
+                        rhs_scale=scales[a][:, first : first + width],
+                        start=(a == 0),
+                        stop=(a == PASSES - 1),
+                    )
+                first = first + width
             columns = keep.tile([P, n], F32, name=f"columns{j0}")
-            nc.scalar.activation(columns[:], acc[:], SILU, bias=b_column[:])
+            nc.scalar.activation(
+                columns[:].rearrange("m (c p) -> m c p", p=P),
+                acc[:].rearrange("m (p c) -> m c p", p=P),
+                SILU,
+                bias=b_column[:],
+            )
             turned = bank(first_bank + 1, [P, n // P, P], f"turned{j0}")
             for c in range(n // P):
                 nc.tensor.transpose(turned[:, c, :], columns[:, c * P : (c + 1) * P], identity[:])
             rows = keep.tile([P, n // P, P], F32, name=f"rows{j0}")
             nc.scalar.copy(rows[:], turned[:])
-            nc.sync.dma_start(out[j0 : j0 + n, :].rearrange("(c p) n -> p c n", p=P), rows[:])
+            nc.sync.dma_start(out[j0 : j0 + n, :].rearrange("(p c) n -> p c n", p=P), rows[:])
 
         def project_direct(store, index, j0, n):
             acc = bank(index, [P, n // P, P], f"acc{j0}")
@@ -175,7 +178,7 @@ def tile_list_heads_tm_silu_kernel(tc, xT, w_words, w_scales, wgt, b, offs, out)
 
         for u0 in (0, 2, 4):
             if u0 < 4:
-                picked = keep.tile([P, 2, S], F32, name=f"picked{u0}")
+                picked = keep.tile([P, 2, S], F32, name=f"picked{u0}", tag=f"picked{u0}")
                 for u in (u0, u0 + 1):
                     for j0, n in PIECES.get(u, [(0, S)]):
                         gather(picked[:, u - u0, j0 : j0 + n], u, j0, n)
@@ -189,39 +192,35 @@ def tile_list_heads_tm_silu_kernel(tc, xT, w_words, w_scales, wgt, b, offs, out)
                 for j0, n in HALVES:
                     interleave(nc.scalar.copy, picked[:, :, j0 : j0 + n], u0, j0, n)
 
-        codes[0, 0] = keep.tile([P, 512], U32, name="codes00", align_bytes=64)
-        quantise(0, 0, 512)
+        b_turned = bank(4, [P, P], "b_turned")
+        nc.tensor.transpose(b_turned[:], b_column[:].to_broadcast([P, P]), identity[:])
+        b_rows = keep.tile([P, P], F32, name="b_rows", tag="picked0")
+        nc.scalar.copy(b_rows[:], b_turned[:])
         codes[1, 0] = keep.tile([P, 512], U32, name="codes10", align_bytes=64)
         codes[1, 1] = keep.tile([P, 512], U32, name="codes11", align_bytes=64)
 
-        def picked_pair(j0, n, slot):
-            return keep.tile([P, 2, n], F32, name=f"pair{j0}", tag=f"ring{slot}")
-
-        front = [picked_pair(256 * q, 256, q) for q in range(2)]
-        for q in range(2):
-            gather(front[q][:, 0, :], 6, 256 * q, 256)
-        gather(front[0][:, 1, :], 7, 0, 256, late_weights[:])
-        gather(front[1][:, 1, :], 7, 256, 256)
-        codes[0, 1] = keep.tile([P, 512], U32, name="codes01", tag="late", align_bytes=64)
+        front = keep.tile([P, 2, 512], F32, name="front", tag="front", align_bytes=64)
+        middle = keep.tile([P, 2, 384], F32, name="middle", tag="pair")
+        gather(front[:, 0, :], 6, 0, 512)
+        gather(middle[:, 0, :], 6, 512, 384)
+        early = [(front, 0, 0, 256), (front, 256, 256, 256), (middle, 0, 512, 256), (middle, 256, 768, 128)]
+        for pair, at, j0, n in early:
+            gather(pair[:, 1, at : at + n], 7, j0, n, late_weights[:] if j0 == 0 else None)
+        codes[0, 0] = keep.tile([P, 512], U32, name="codes00", tag="late", align_bytes=64)
+        quantise(0, 0, 512)
+        for pair, at, j0, n in early:
+            interleave(nc.scalar.copy, pair[:, :, at : at + n], 6, j0, n)
+        quantise(1, 0, 512)
+        codes[0, 1] = keep.tile([P, 512], U32, name="codes01", tag="front", align_bytes=64)
         quantise(0, 512, 512)
-        for q in (0, 1):
-            interleave(nc.scalar.copy, front[q][:], 6, 256 * q, 256)
-            quantise(1, 256 * q, 256)
-            project_turned(2 * q, 256 * q, 256)
+        for j0, n in [(512, 256), (768, 128)]:
+            quantise(1, j0, n)
+        project_turned(0, 0, [512])
+        project_turned(2, 512, [256, 128])
 
-        third = picked_pair(512, 256, 0)
+        last = keep.tile([P, 2, P], F32, name="last", tag="pair")
         for u in (6, 7):
-            gather(third[:, u - 6, :], u, 512, 256)
-        interleave(nc.scalar.copy, third[:], 6, 512, 256)
-        quantise(1, 512, 256)
-        project_direct(nc.sync.dma_start, 4, 512, 256)
-
-        fourth = picked_pair(768, 256, 1)
-        gather(fourth[:, 0, :], 6, 768, 256)
-        for c in range(2):
-            gather(fourth[:, 1, c * P : (c + 1) * P], 7, 768 + c * P, P)
-        for c, (copy, store) in enumerate([(nc.scalar.copy, nc.sync.dma_start), (nc.vector.tensor_copy, nc.scalar.dma_start)]):
-            j0 = 768 + c * P
-            interleave(copy, fourth[:, :, c * P : (c + 1) * P], 6, j0, P)
-            quantise(1, j0, P)
-            project_direct(store, 6 + c, j0, P)
+            gather(last[:, u - 6, :], u, 896, P)
+        interleave(nc.vector.tensor_copy, last[:], 6, 896, P)
+        quantise(1, 896, P)
+        project_direct(nc.scalar.dma_start, 7, 896, P)

@@ -27,9 +27,8 @@ GROUPS = P // LANES
 BLOCKS = S // P
 
 HALVES = [(0, 512), (512, 512)]
-QUARTERS = [(j0, 256) for j0 in range(0, S, 256)]
 WEIGHT_PIECES = [(0, 128), (128, 128), (256, 256), (512, 256), (768, 256)]
-PIECES = {0: [(0, 128), (128, 384), (512, 512)], 5: HALVES}
+PIECES = {0: [(0, 128), (128, 384), (512, 512)], 3: HALVES, 5: HALVES}
 
 
 def tile_list_heads_tm_silu_kernel(tc, xT, w_words, w_scales, wgt, b, offs, out):
@@ -71,7 +70,7 @@ def tile_list_heads_tm_silu_kernel(tc, xT, w_words, w_scales, wgt, b, offs, out)
         nc.sync.dma_start(w_codes[:].bitcast(I32), w_words.rearrange("a p n i -> p a (n i)").bitcast(I32))
         scale_source = w_scales.bitcast(I32).rearrange("a q n -> q a n")
         for quadrant in range(4):
-            nc.sync.dma_start(
+            nc.gpsimd.dma_start(
                 w_scale_rows[32 * quadrant : 32 * quadrant + 4].bitcast(I32),
                 scale_source[4 * quadrant : 4 * quadrant + 4],
             )
@@ -79,7 +78,6 @@ def tile_list_heads_tm_silu_kernel(tc, xT, w_words, w_scales, wgt, b, offs, out)
         small_columns = bank(7, [P, P], "small_columns")
         nc.tensor.transpose(small_columns[:], small_rows[:], identity[:])
         token_weights = keep.tile([P, S], F32, name="token_weights")
-        late_weights = keep.tile([P, 256], F32, name="late_weights", tag="late", align_bytes=64)
         for q, (j0, n) in enumerate(WEIGHT_PIECES):
             columns = n // P * GROUPS
             spread = keep.tile([P, columns, LANES], F32, name=f"spread{q}")
@@ -95,16 +93,16 @@ def tile_list_heads_tm_silu_kernel(tc, xT, w_words, w_scales, wgt, b, offs, out)
                     identity[:],
                 )
             nc.scalar.copy(token_weights[:, j0 : j0 + n], turned_back[:])
-        nc.scalar.copy(late_weights[:], token_weights[:, 0:256])
         grouped = [keep.tile([P, S, PACK], BF16, name=f"grouped{a}", align_bytes=64) for a in range(PASSES)]
-        codes = {}
         scales = [keep.tile([P, S], U8, name=f"scales{a}", align_bytes=64) for a in range(PASSES)]
+        codes = [keep.tile([P, S], U32, name=f"codes{a}", align_bytes=64) for a in range(PASSES)]
+        apart = {}
 
-        def gather(picked, u, j0, n, weights=None):
+        def gather(picked, u, j0, n):
             nc.vector.tensor_tensor(
                 picked,
                 planes[u][:].indirect(offsets[:, j0 // LANES : (j0 + n) // LANES]),
-                token_weights[:, j0 : j0 + n] if weights is None else weights,
+                token_weights[:, j0 : j0 + n],
                 MULT,
             )
 
@@ -116,8 +114,10 @@ def tile_list_heads_tm_silu_kernel(tc, xT, w_words, w_scales, wgt, b, offs, out)
             )
 
         def codes_of(a, j0, n):
-            half = j0 // 512
-            return codes[a, half][:, j0 - 512 * half : j0 - 512 * half + n].bitcast(FP8X4)
+            for (pass_apart, begin), tile_apart in apart.items():
+                if pass_apart == a and j0 >= begin:
+                    return tile_apart[:, j0 - begin : j0 - begin + n].bitcast(FP8X4)
+            return codes[a][:, j0 : j0 + n].bitcast(FP8X4)
 
         def quantise(a, j0, n):
             nc.vector.quantize_mx(
@@ -126,22 +126,18 @@ def tile_list_heads_tm_silu_kernel(tc, xT, w_words, w_scales, wgt, b, offs, out)
                 in_=grouped[a][:, j0 : j0 + n, :].rearrange("p j i -> p (j i)"),
             )
 
-        def project_turned(first_bank, j0, pieces):
-            n = sum(pieces)
-            acc = bank(first_bank, [P, n], f"acc{j0}")
-            first = j0
-            for width in pieces:
-                for a in range(PASSES):
-                    nc.tensor.matmul_mx(
-                        out=acc[:, first - j0 : first - j0 + width],
-                        lhsT=w_codes[:, a, :].bitcast(FP8X4),
-                        lhsT_scale=w_scale_rows[:, a, :],
-                        rhs=codes_of(a, first, width),
-                        rhs_scale=scales[a][:, first : first + width],
-                        start=(a == 0),
-                        stop=(a == PASSES - 1),
-                    )
-                first = first + width
+        def pass_turned(acc, a, j0, n):
+            nc.tensor.matmul_mx(
+                out=acc[:],
+                lhsT=w_codes[:, a, :].bitcast(FP8X4),
+                lhsT_scale=w_scale_rows[:, a, :],
+                rhs=codes_of(a, j0, n),
+                rhs_scale=scales[a][:, j0 : j0 + n],
+                start=(a == 0),
+                stop=(a == PASSES - 1),
+            )
+
+        def silu_turned(acc, j0, n):
             columns = keep.tile([P, n], F32, name=f"columns{j0}")
             nc.scalar.activation(
                 columns[:].rearrange("m (c p) -> m c p", p=P),
@@ -149,78 +145,98 @@ def tile_list_heads_tm_silu_kernel(tc, xT, w_words, w_scales, wgt, b, offs, out)
                 SILU,
                 bias=b_column[:],
             )
-            turned = bank(first_bank + 1, [P, n // P, P], f"turned{j0}")
+            return columns
+
+        def turn(columns, index, j0, n):
+            turned = bank(index, [P, n // P, P], f"turned{j0}")
             for c in range(n // P):
                 nc.tensor.transpose(turned[:, c, :], columns[:, c * P : (c + 1) * P], identity[:])
+            return turned
+
+        def store_turned(turned, j0, n):
             rows = keep.tile([P, n // P, P], F32, name=f"rows{j0}")
             nc.scalar.copy(rows[:], turned[:])
             nc.sync.dma_start(out[j0 : j0 + n, :].rearrange("(p c) n -> p c n", p=P), rows[:])
 
-        def project_direct(store, index, j0, n):
-            acc = bank(index, [P, n // P, P], f"acc{j0}")
-            for c in range(n // P):
-                first = j0 + c * P
-                for a in range(PASSES):
-                    nc.tensor.matmul_mx(
-                        out=acc[:, c, :],
-                        lhsT=codes_of(a, first, P),
-                        lhsT_scale=scales[a][:, first : first + P],
-                        rhs=w_codes[:, a, :].bitcast(FP8X4),
-                        rhs_scale=w_scale_rows[:, a, :],
-                        start=(a == 0),
-                        stop=(a == PASSES - 1),
-                    )
-            biased = keep.tile([P, n // P, P], F32, name=f"biased{j0}")
-            nc.vector.tensor_tensor(biased[:], acc[:], b_rows[:].unsqueeze(1).to_broadcast([P, n // P, P]), ADD)
+        def pass_direct(acc, a, j0, c, blocks):
+            first = j0 + c * P
+            nc.tensor.matmul_mx(
+                out=acc[:, c, :],
+                lhsT=codes_of(a, first, P),
+                lhsT_scale=scales[a][:, first : first + P],
+                rhs=w_codes[:, a, :].bitcast(FP8X4),
+                rhs_scale=w_scale_rows[:, a, :],
+                start=(a == 0 and c == 0),
+                stop=(a == PASSES - 1 and c == blocks - 1),
+            )
+
+        def add_bias(biased, acc, n):
+            nc.vector.tensor_tensor(biased, acc[:], b_rows[:].unsqueeze(1).to_broadcast([P, n // P, P]), ADD)
+
+        def store_direct(store, biased, j0, n):
             rows = keep.tile([P, n // P, P], F32, name=f"rows{j0}")
-            nc.scalar.activation(rows[:], biased[:], SILU)
+            nc.scalar.activation(rows[:], biased, SILU)
             store(out[j0 : j0 + n, :].rearrange("(c p) n -> p c n", p=P), rows[:])
 
         for u0 in (0, 2, 4):
-            if u0 < 4:
-                picked = keep.tile([P, 2, S], F32, name=f"picked{u0}", tag=f"picked{u0}")
-                for u in (u0, u0 + 1):
-                    for j0, n in PIECES.get(u, [(0, S)]):
-                        gather(picked[:, u - u0, j0 : j0 + n], u, j0, n)
-                for j0, n in HALVES if u0 == 2 else [(0, S)]:
-                    interleave(nc.scalar.copy, picked[:, :, j0 : j0 + n], u0, j0, n)
-            else:
-                picked = keep.tile([P, 2, S], F32, name=f"picked{u0}")
-                gather(picked[:, 0, :], 4, 0, S)
-                for j0, n in HALVES:
-                    gather(picked[:, 1, j0 : j0 + n], 5, j0, n)
-                for j0, n in HALVES:
-                    interleave(nc.scalar.copy, picked[:, :, j0 : j0 + n], u0, j0, n)
+            picked = keep.tile([P, 2, S], F32, name=f"picked{u0}", tag=f"picked{u0}", align_bytes=64)
+            for u in (u0, u0 + 1):
+                for j0, n in PIECES.get(u, [(0, S)]):
+                    gather(picked[:, u - u0, j0 : j0 + n], u, j0, n)
+            for j0, n in HALVES if u0 > 0 else [(0, S)]:
+                interleave(nc.scalar.copy, picked[:, :, j0 : j0 + n], u0, j0, n)
 
         b_turned = bank(4, [P, P], "b_turned")
         nc.tensor.transpose(b_turned[:], b_column[:].to_broadcast([P, P]), identity[:])
-        b_rows = keep.tile([P, P], F32, name="b_rows", tag="picked0")
+        b_rows = keep.tile([P, P], F32, name="b_rows", tag="picked0", align_bytes=64)
         nc.scalar.copy(b_rows[:], b_turned[:])
-        codes[1, 0] = keep.tile([P, 512], U32, name="codes10", align_bytes=64)
-        codes[1, 1] = keep.tile([P, 512], U32, name="codes11", align_bytes=64)
 
-        front = keep.tile([P, 2, 512], F32, name="front", tag="front", align_bytes=64)
-        middle = keep.tile([P, 2, 384], F32, name="middle", tag="pair")
-        gather(front[:, 0, :], 6, 0, 512)
-        gather(middle[:, 0, :], 6, 512, 384)
-        early = [(front, 0, 0, 256), (front, 256, 256, 256), (middle, 0, 512, 256), (middle, 256, 768, 128)]
-        for pair, at, j0, n in early:
-            gather(pair[:, 1, at : at + n], 7, j0, n, late_weights[:] if j0 == 0 else None)
-        codes[0, 0] = keep.tile([P, 512], U32, name="codes00", tag="late", align_bytes=64)
         quantise(0, 0, 512)
-        for pair, at, j0, n in early:
-            interleave(nc.scalar.copy, pair[:, :, at : at + n], 6, j0, n)
-        quantise(1, 0, 512)
-        codes[0, 1] = keep.tile([P, 512], U32, name="codes01", tag="front", align_bytes=64)
         quantise(0, 512, 512)
-        for j0, n in [(512, 256), (768, 128)]:
-            quantise(1, j0, n)
-        project_turned(0, 0, [512])
-        project_turned(2, 512, [256, 128])
+        late = keep.tile([P, 2048], F32, name="late", tag="late", align_bytes=64)
 
-        last = keep.tile([P, 2, P], F32, name="last", tag="pair")
-        for u in (6, 7):
-            gather(last[:, u - 6, :], u, 896, P)
-        interleave(nc.vector.tensor_copy, last[:], 6, 896, P)
-        quantise(1, 896, P)
-        project_direct(nc.scalar.dma_start, 7, 896, P)
+        def pair_of(j0, n):
+            return late[:].rearrange("p (i j) -> p i j", i=2)[:, :, 256 + j0 : 256 + j0 + n]
+
+        gather(late[:, 256:1024], 6, 0, 768)
+        gather(late[:, 0:256], 6, 768, 256)
+        for j0 in (0, 256, 512):
+            gather(late[:, 1280 + j0 : 1536 + j0], 7, j0, 256)
+        for j0 in (0, 256, 512):
+            interleave(nc.scalar.copy, pair_of(j0, 256), 6, j0, 256)
+        acc_a = bank(0, [P, 256], "acc_a")
+        acc_b = bank(1, [P, 2, P], "acc_b")
+        acc_c = bank(6, [P, 2, P], "acc_c")
+        acc_d = bank(5, [P, 2, P], "acc_d")
+        pass_turned(acc_a, 0, 0, 256)
+        for acc, j0 in ((acc_b, 256), (acc_c, 512), (acc_d, 768)):
+            for c in range(2):
+                pass_direct(acc, 0, j0, c, 2)
+        quantise(1, 0, 256)
+        gather(late[:, 384:512], 7, 768, P)
+        gather(late[:, 512:640], 7, 896, P)
+        quantise(1, 256, 256)
+        interleave(
+            nc.vector.tensor_copy, late[:, 0:768].rearrange("p (i j) -> p i j", i=2)[:, :, 0:256], 6, 768, 256
+        )
+        quantise(1, 512, 256)
+        apart[1, 768] = keep.tile([P, 256], U32, name="codes_last", tag="late", align_bytes=64)
+        quantise(1, 768, 256)
+        pass_turned(acc_a, 1, 0, 256)
+        columns_a = silu_turned(acc_a, 0, 256)
+        for c in range(2):
+            pass_direct(acc_b, 1, 256, c, 2)
+        turned_a = turn(columns_a, 2, 0, 256)
+        for acc, j0 in ((acc_c, 512), (acc_d, 768)):
+            for c in range(2):
+                pass_direct(acc, 1, j0, c, 2)
+        store_turned(turned_a, 0, 256)
+        biased_b = grouped[1][:, 512:640, :].rearrange("p j i -> p (j i)").bitcast(F32).rearrange("p (c n) -> p c n", n=P)
+        biased_c = keep.tile([P, 2, P], F32, name="biased_c")
+        biased_d = keep.tile([P, 2, P], F32, name="biased_d")
+        add_bias(biased_b, acc_b, 256)
+        add_bias(biased_c[:], acc_c, 256)
+        add_bias(biased_d[:], acc_d, 256)
+        store_direct(nc.sync.dma_start, biased_b, 256, 256)
+        store_direct(nc.sync.dma_start, biased_c[:], 512, 256)
+        store_direct(nc.scalar.dma_start, biased_d[:], 768, 256)

@@ -42,9 +42,9 @@ def tile_list_heads_tm_silu_kernel(tc, xT, w_words, w_scales, wgt, b, offs, out)
 
         small_rows = keep.tile([P, P], F32, name="small_rows")
         nc.vector.memset(small_rows[64:128, :], 0.0)
-        nc.sync.dma_start(
-            small_rows[0:64, :], wgt.rearrange("(g l) (h j) -> l h g j", l=LANES, j=P)[0]
-        )
+        stride = 7 * S + S // 2
+        halves = wgt.rearrange("r j -> (r j)")[7 * S : 7 * S + 16 * stride].rearrange("(q j) -> q j", q=16)
+        nc.sync.dma_start(small_rows[0:64, :], halves[:, 0 : S // 2].rearrange("q (h j) -> q h j", j=P))
 
         plane_rows = xT.rearrange("(a p i) t -> a i p t", p=P, i=PACK)
         planes = [keep.tile([P, T], F32, name=f"plane{u}", tag=f"plane{u}", align_bytes=64) for u in range(PLANES)]
@@ -52,13 +52,14 @@ def tile_list_heads_tm_silu_kernel(tc, xT, w_words, w_scales, wgt, b, offs, out)
         w_codes = keep.tile([P, PASSES, M], U32, name="w_codes", align_bytes=64)
         w_scale_rows = keep.tile([P, PASSES, M], U8, name="w_scale_rows", align_bytes=64)
 
-        b_column = keep.tile([P, 1], F32, name="b_column")
+        b_row = keep.tile([P, P], F32, name="b_row")
+        nc.vector.memset(b_row[:], 0.0)
         for u in range(PLANES):
             nc.sync.dma_start(planes[u][:], plane_rows[u // PACK, u % PACK])
             if u == 0:
                 nc.sync.dma_start(offsets[:], offs)
-            if u == 3:
-                nc.sync.dma_start(b_column[:], b.rearrange("(p o) -> p o", o=1))
+            if u == 1:
+                nc.sync.dma_start(b_row[0:1, :], b.rearrange("(o n) -> o n", o=1))
 
         identity = keep.tile([P, P], F32, name="identity")
         make_identity(nc, identity[:])
@@ -79,17 +80,17 @@ def tile_list_heads_tm_silu_kernel(tc, xT, w_words, w_scales, wgt, b, offs, out)
         nc.tensor.transpose(small_columns[:], small_rows[:], identity[:])
         token_weights = keep.tile([P, S], F32, name="token_weights")
         for q, (j0, n) in enumerate(WEIGHT_PIECES):
-            columns = n // P * GROUPS
-            spread = keep.tile([P, columns, LANES], F32, name=f"spread{q}")
-            first = j0 // P * GROUPS
+            spread = keep.tile([P, n // P, GROUPS, LANES], F32, name=f"spread{q}")
+            by_block = small_columns[:, 0 : GROUPS * BLOCKS].rearrange("p (g k) -> p k g", g=GROUPS)
             nc.vector.tensor_copy(
-                spread[:], small_columns[:, first : first + columns].unsqueeze(2).to_broadcast([P, columns, LANES])
+                spread[:],
+                by_block[:, j0 // P : (j0 + n) // P, :].unsqueeze(3).to_broadcast([P, n // P, GROUPS, LANES]),
             )
             turned_back = bank(q, [P, n], f"turned_back{q}")
             for c in range(n // P):
                 nc.tensor.transpose(
                     turned_back[:, c * P : (c + 1) * P],
-                    spread[:].rearrange("p a l -> p (a l)")[:, c * P : (c + 1) * P],
+                    spread[:, c].rearrange("p g l -> p (g l)"),
                     identity[:],
                 )
             nc.scalar.copy(token_weights[:, j0 : j0 + n], turned_back[:])
@@ -186,57 +187,61 @@ def tile_list_heads_tm_silu_kernel(tc, xT, w_words, w_scales, wgt, b, offs, out)
             for j0, n in HALVES if u0 > 0 else [(0, S)]:
                 interleave(nc.scalar.copy, picked[:, :, j0 : j0 + n], u0, j0, n)
 
+        b_upright = bank(4, [P, P], "b_upright")
+        nc.tensor.transpose(b_upright[:], b_row[:], identity[:])
+        b_column = keep.tile([P, 1], F32, name="b_column", tag="picked0", align_bytes=64)
+        nc.scalar.copy(b_column[:], b_upright[:, 0:1])
         b_turned = bank(4, [P, P], "b_turned")
         nc.tensor.transpose(b_turned[:], b_column[:].to_broadcast([P, P]), identity[:])
-        b_rows = keep.tile([P, P], F32, name="b_rows", tag="picked0", align_bytes=64)
+        b_rows = keep.tile([P, P], F32, name="b_rows")
         nc.scalar.copy(b_rows[:], b_turned[:])
 
         quantise(0, 0, 512)
         quantise(0, 512, 512)
-        late = keep.tile([P, 2048], F32, name="late", tag="late", align_bytes=64)
-
-        def pair_of(j0, n):
-            return late[:].rearrange("p (i j) -> p i j", i=2)[:, :, 256 + j0 : 256 + j0 + n]
-
-        gather(late[:, 256:1024], 6, 0, 768)
-        gather(late[:, 0:256], 6, 768, 256)
+        late = keep.tile([P, 2, 768], F32, name="late")
+        gather(late[:, 0, :], 6, 0, 768)
         for j0 in (0, 256, 512):
-            gather(late[:, 1280 + j0 : 1536 + j0], 7, j0, 256)
+            gather(late[:, 1, j0 : j0 + 256], 7, j0, 256)
         for j0 in (0, 256, 512):
-            interleave(nc.scalar.copy, pair_of(j0, 256), 6, j0, 256)
+            interleave(nc.scalar.copy, late[:, :, j0 : j0 + 256], 6, j0, 256)
         acc_a = bank(0, [P, 256], "acc_a")
-        acc_b = bank(1, [P, 2, P], "acc_b")
+        acc_b = bank(1, [P, 256], "acc_b")
         acc_c = bank(6, [P, 2, P], "acc_c")
-        acc_d = bank(5, [P, 2, P], "acc_d")
+        acc_d = bank(5, [P, 1, P], "acc_d")
+        acc_e = bank(7, [P, 1, P], "acc_e")
         pass_turned(acc_a, 0, 0, 256)
-        for acc, j0 in ((acc_b, 256), (acc_c, 512), (acc_d, 768)):
-            for c in range(2):
-                pass_direct(acc, 0, j0, c, 2)
+        pass_turned(acc_b, 0, 256, 256)
+        pass_direct(acc_c, 0, 512, 0, 2)
+        pass_direct(acc_c, 0, 512, 1, 2)
+        pass_direct(acc_d, 0, 768, 0, 1)
+        pass_direct(acc_e, 0, 896, 0, 1)
+        back = late[:, 0, 0:512].rearrange("p (i j) -> p i j", i=2)
         quantise(1, 0, 256)
-        gather(late[:, 384:512], 7, 768, P)
-        gather(late[:, 512:640], 7, 896, P)
+        gather(back[:, 0, :], 6, 768, 256)
         quantise(1, 256, 256)
-        interleave(
-            nc.vector.tensor_copy, late[:, 0:768].rearrange("p (i j) -> p i j", i=2)[:, :, 0:256], 6, 768, 256
-        )
+        gather(back[:, 1, 0:P], 7, 768, P)
+        gather(back[:, 1, P:256], 7, 896, P)
         quantise(1, 512, 256)
-        apart[1, 768] = keep.tile([P, 256], U32, name="codes_last", tag="late", align_bytes=64)
-        quantise(1, 768, 256)
+        interleave(nc.vector.tensor_copy, back[:, :, 0:P], 6, 768, P)
+        interleave(nc.vector.tensor_copy, back[:, :, P:256], 6, 896, P)
+        quantise(1, 768, P)
+        quantise(1, 896, P)
         pass_turned(acc_a, 1, 0, 256)
+        pass_turned(acc_b, 1, 256, 256)
         columns_a = silu_turned(acc_a, 0, 256)
-        for c in range(2):
-            pass_direct(acc_b, 1, 256, c, 2)
+        columns_b = silu_turned(acc_b, 256, 256)
         turned_a = turn(columns_a, 2, 0, 256)
-        for acc, j0 in ((acc_c, 512), (acc_d, 768)):
-            for c in range(2):
-                pass_direct(acc, 1, j0, c, 2)
+        turned_b = turn(columns_b, 3, 256, 256)
+        for c in range(2):
+            pass_direct(acc_c, 1, 512, c, 2)
+        pass_direct(acc_d, 1, 768, 0, 1)
+        pass_direct(acc_e, 1, 896, 0, 1)
         store_turned(turned_a, 0, 256)
-        biased_b = grouped[1][:, 512:640, :].rearrange("p j i -> p (j i)").bitcast(F32).rearrange("p (c n) -> p c n", n=P)
-        biased_c = keep.tile([P, 2, P], F32, name="biased_c")
-        biased_d = keep.tile([P, 2, P], F32, name="biased_d")
-        add_bias(biased_b, acc_b, 256)
-        add_bias(biased_c[:], acc_c, 256)
-        add_bias(biased_d[:], acc_d, 256)
-        store_direct(nc.sync.dma_start, biased_b, 256, 256)
-        store_direct(nc.sync.dma_start, biased_c[:], 512, 256)
-        store_direct(nc.scalar.dma_start, biased_d[:], 768, 256)
+        store_turned(turned_b, 256, 256)
+        biased_c = grouped[1][:, 768:896, :].rearrange("p j i -> p (j i)").bitcast(F32).rearrange("p (c n) -> p c n", n=P)
+        biased_last = keep.tile([P, 2, P], F32, name="biased_last")
+        add_bias(biased_c, acc_c, 256)
+        add_bias(biased_last[:, 0:1, :], acc_d, P)
+        add_bias(biased_last[:, 1:2, :], acc_e, P)
+        store_direct(nc.sync.dma_start, biased_c, 512, 256)
+        store_direct(nc.scalar.dma_start, biased_last[:], 768, 256)

@@ -80,7 +80,7 @@ def tile_list_heads_tm_silu_kernel(tc, xT, w_words, w_scales, wgt, b, offs, out)
         nc.tensor.transpose(small_columns[:], small_rows[:], identity[:])
         token_weights = keep.tile([P, S], F32, name="token_weights")
         for q, (j0, n) in enumerate(WEIGHT_PIECES):
-            spread = keep.tile([P, n // P, GROUPS, LANES], F32, name=f"spread{q}")
+            spread = keep.tile([P, n // P, GROUPS, LANES], F32, name=f"spread{q}", tag=f"spread{q}", align_bytes=64)
             by_block = small_columns[:, 0 : GROUPS * BLOCKS].rearrange("p (g k) -> p k g", g=GROUPS)
             nc.vector.tensor_copy(
                 spread[:],
@@ -94,16 +94,19 @@ def tile_list_heads_tm_silu_kernel(tc, xT, w_words, w_scales, wgt, b, offs, out)
                     identity[:],
                 )
             nc.scalar.copy(token_weights[:, j0 : j0 + n], turned_back[:])
+        first_weights = keep.tile([P, 512], F32, name="first_weights", tag="spread4", align_bytes=64)
+        nc.scalar.copy(first_weights[:], token_weights[:, 0:512])
+
         grouped = [keep.tile([P, S, PACK], BF16, name=f"grouped{a}", align_bytes=64) for a in range(PASSES)]
         scales = [keep.tile([P, S], U8, name=f"scales{a}", align_bytes=64) for a in range(PASSES)]
         codes = [keep.tile([P, S], U32, name=f"codes{a}", align_bytes=64) for a in range(PASSES)]
         apart = {}
 
-        def gather(picked, u, j0, n):
+        def gather(picked, u, j0, n, weights=None):
             nc.vector.tensor_tensor(
                 picked,
                 planes[u][:].indirect(offsets[:, j0 // LANES : (j0 + n) // LANES]),
-                token_weights[:, j0 : j0 + n],
+                token_weights[:, j0 : j0 + n] if weights is None else weights,
                 MULT,
             )
 
@@ -197,11 +200,12 @@ def tile_list_heads_tm_silu_kernel(tc, xT, w_words, w_scales, wgt, b, offs, out)
         nc.scalar.copy(b_rows[:], b_turned[:])
 
         quantise(0, 0, 512)
-        quantise(0, 512, 512)
         late = keep.tile([P, 2, 768], F32, name="late")
         gather(late[:, 0, :], 6, 0, 768)
         for j0 in (0, 256, 512):
-            gather(late[:, 1, j0 : j0 + 256], 7, j0, 256)
+            gather(late[:, 1, j0 : j0 + 256], 7, j0, 256, first_weights[:, j0 : j0 + 256] if j0 < 512 else None)
+        apart[0, 512] = keep.tile([P, 512], U32, name="codes_late", tag="spread4", align_bytes=64)
+        quantise(0, 512, 512)
         for j0 in (0, 256, 512):
             interleave(nc.scalar.copy, late[:, :, j0 : j0 + 256], 6, j0, 256)
         acc_a = bank(0, [P, 256], "acc_a")
@@ -211,10 +215,6 @@ def tile_list_heads_tm_silu_kernel(tc, xT, w_words, w_scales, wgt, b, offs, out)
         acc_e = bank(7, [P, 1, P], "acc_e")
         pass_turned(acc_a, 0, 0, 256)
         pass_turned(acc_b, 0, 256, 256)
-        pass_direct(acc_c, 0, 512, 0, 2)
-        pass_direct(acc_c, 0, 512, 1, 2)
-        pass_direct(acc_d, 0, 768, 0, 1)
-        pass_direct(acc_e, 0, 896, 0, 1)
         back = late[:, 0, 0:512].rearrange("p (i j) -> p i j", i=2)
         quantise(1, 0, 256)
         gather(back[:, 0, :], 6, 768, 256)
@@ -227,6 +227,10 @@ def tile_list_heads_tm_silu_kernel(tc, xT, w_words, w_scales, wgt, b, offs, out)
         quantise(1, 768, P)
         quantise(1, 896, P)
         pass_turned(acc_a, 1, 0, 256)
+        pass_direct(acc_c, 0, 512, 0, 2)
+        pass_direct(acc_c, 0, 512, 1, 2)
+        pass_direct(acc_d, 0, 768, 0, 1)
+        pass_direct(acc_e, 0, 896, 0, 1)
         pass_turned(acc_b, 1, 256, 256)
         columns_a = silu_turned(acc_a, 0, 256)
         columns_b = silu_turned(acc_b, 256, 256)

@@ -50,7 +50,8 @@ def tile_list_heads_tm_silu_kernel(tc, xT, w_words, w_scales, wgt, b, offs, out)
         planes = [keep.tile([P, T], F32, name=f"plane{u}", tag=f"plane{u}", align_bytes=64) for u in range(PLANES)]
         offsets = keep.tile([P, S // LANES], U16, name="offsets")
         w_codes = keep.tile([P, PASSES, M], U32, name="w_codes", align_bytes=64)
-        w_scale_rows = keep.tile([P, PASSES, M], U8, name="w_scale_rows", align_bytes=64)
+        shared_planes = keep.tile([P, 512], U8, name="shared_planes", align_bytes=64)
+        w_scale_rows = shared_planes[:, 0 : PASSES * M].rearrange("p (a n) -> p a n", a=PASSES)
 
         b_row = keep.tile([P, P], F32, name="b_row")
         nc.vector.memset(b_row[:], 0.0)
@@ -66,7 +67,7 @@ def tile_list_heads_tm_silu_kernel(tc, xT, w_words, w_scales, wgt, b, offs, out)
         warm_up = keep.tile([P, 1], F32, name="warm_up")
         nc.vector.memset(warm_up[:], 0.0)
         nc.scalar.activation(warm_up[:], warm_up[:], SILU)
-        nc.vector.memset(w_scale_rows[:].rearrange("p a n -> p (a n)").bitcast(I32), 0)
+        nc.vector.memset(shared_planes[:].bitcast(I32), 0)
 
         nc.sync.dma_start(w_codes[:].bitcast(I32), w_words.rearrange("a p n i -> p a (n i)").bitcast(I32))
         scale_source = w_scales.bitcast(I32).rearrange("a q n -> q a n")
@@ -113,8 +114,15 @@ def tile_list_heads_tm_silu_kernel(tc, xT, w_words, w_scales, wgt, b, offs, out)
         def interleave(copy, picked, u, j0, n):
             i0 = u % PACK
             copy(
-                grouped[u // PACK][:, j0 : j0 + n, i0 : i0 + picked.shape[1]],
-                picked.rearrange("p i j -> p j i"),
+                grouped[u // PACK][:, j0 : j0 + n, i0 : i0 + 2].rearrange("p (s c t) i -> p s c t i", c=2, t=P),
+                picked.rearrange("p i (s t c) -> p s c t i", c=2, t=P),
+            )
+
+        def interleave_half(copy, picked, u, j0, c):
+            i0 = u % PACK
+            copy(
+                grouped[u // PACK][:, j0 + c * P : j0 + (c + 1) * P, i0 : i0 + 2],
+                picked.rearrange("p i (t c) -> p c t i", c=2)[:, c],
             )
 
         def codes_of(a, j0, n):
@@ -123,10 +131,15 @@ def tile_list_heads_tm_silu_kernel(tc, xT, w_words, w_scales, wgt, b, offs, out)
                     return tile_apart[:, j0 - begin : j0 - begin + n].bitcast(FP8X4)
             return codes[a][:, j0 : j0 + n].bitcast(FP8X4)
 
+        def scales_of(a, j0, n):
+            if a == 0 and j0 >= 512:
+                return shared_planes[4:P, j0 - 512 : j0 - 512 + n]
+            return scales[a][:, j0 : j0 + n]
+
         def quantise(a, j0, n):
             nc.vector.quantize_mx(
                 out=codes_of(a, j0, n),
-                scales=scales[a][:, j0 : j0 + n],
+                scales=scales_of(a, j0, n),
                 in_=grouped[a][:, j0 : j0 + n, :].rearrange("p j i -> p (j i)"),
             )
 
@@ -136,19 +149,14 @@ def tile_list_heads_tm_silu_kernel(tc, xT, w_words, w_scales, wgt, b, offs, out)
                 lhsT=w_codes[:, a, :].bitcast(FP8X4),
                 lhsT_scale=w_scale_rows[:, a, :],
                 rhs=codes_of(a, j0, n),
-                rhs_scale=scales[a][:, j0 : j0 + n],
+                rhs_scale=scales_of(a, j0, n),
                 start=(a == 0),
                 stop=(a == PASSES - 1),
             )
 
         def silu_turned(acc, j0, n):
             columns = keep.tile([P, n], F32, name=f"columns{j0}")
-            nc.scalar.activation(
-                columns[:].rearrange("m (c p) -> m c p", p=P),
-                acc[:].rearrange("m (p c) -> m c p", p=P),
-                SILU,
-                bias=b_column[:],
-            )
+            nc.scalar.activation(columns[:], acc[:], SILU, bias=b_column[:])
             return columns
 
         def turn(columns, index, j0, n):
@@ -167,7 +175,7 @@ def tile_list_heads_tm_silu_kernel(tc, xT, w_words, w_scales, wgt, b, offs, out)
             nc.tensor.matmul_mx(
                 out=acc[:, c, :],
                 lhsT=codes_of(a, first, P),
-                lhsT_scale=scales[a][:, first : first + P],
+                lhsT_scale=scales_of(a, first, P),
                 rhs=w_codes[:, a, :].bitcast(FP8X4),
                 rhs_scale=w_scale_rows[:, a, :],
                 start=(a == 0 and c == 0),
@@ -180,7 +188,7 @@ def tile_list_heads_tm_silu_kernel(tc, xT, w_words, w_scales, wgt, b, offs, out)
         def store_direct(store, biased, j0, n):
             rows = keep.tile([P, n // P, P], F32, name=f"rows{j0}")
             nc.scalar.activation(rows[:], biased, SILU)
-            store(out[j0 : j0 + n, :].rearrange("(c p) n -> p c n", p=P), rows[:])
+            store(out[j0 : j0 + n, :].rearrange("(p c) n -> p c n", p=P), rows[:])
 
         for u0 in (0, 2, 4):
             picked = keep.tile([P, 2, S], F32, name=f"picked{u0}", tag=f"picked{u0}", align_bytes=64)
@@ -214,22 +222,21 @@ def tile_list_heads_tm_silu_kernel(tc, xT, w_words, w_scales, wgt, b, offs, out)
         acc_d = bank(5, [P, 1, P], "acc_d")
         acc_e = bank(7, [P, 1, P], "acc_e")
         pass_turned(acc_a, 0, 0, 256)
-        pass_turned(acc_b, 0, 256, 256)
+        pass_direct(acc_c, 0, 512, 0, 2)
+        pass_direct(acc_c, 0, 512, 1, 2)
+        pass_direct(acc_d, 0, 768, 0, 1)
         back = late[:, 0, 0:512].rearrange("p (i j) -> p i j", i=2)
         quantise(1, 0, 256)
         gather(back[:, 0, :], 6, 768, 256)
         quantise(1, 256, 256)
-        gather(back[:, 1, 0:P], 7, 768, P)
-        gather(back[:, 1, P:256], 7, 896, P)
+        gather(back[:, 1, :], 7, 768, 256)
         quantise(1, 512, 256)
-        interleave(nc.vector.tensor_copy, back[:, :, 0:P], 6, 768, P)
-        interleave(nc.vector.tensor_copy, back[:, :, P:256], 6, 896, P)
+        interleave_half(nc.vector.tensor_copy, back, 6, 768, 0)
+        interleave_half(nc.vector.tensor_copy, back, 6, 768, 1)
         quantise(1, 768, P)
         quantise(1, 896, P)
         pass_turned(acc_a, 1, 0, 256)
-        pass_direct(acc_c, 0, 512, 0, 2)
-        pass_direct(acc_c, 0, 512, 1, 2)
-        pass_direct(acc_d, 0, 768, 0, 1)
+        pass_turned(acc_b, 0, 256, 256)
         pass_direct(acc_e, 0, 896, 0, 1)
         pass_turned(acc_b, 1, 256, 256)
         columns_a = silu_turned(acc_a, 0, 256)

@@ -22,10 +22,11 @@ PACK = 4
 PASSES = K // (P * PACK)
 PLANES = PASSES * PACK
 LANES = 16
-
 GROUPS = P // LANES
 BLOCKS = S // P
 
+SLICE = 256
+SLICES = S // SLICE
 HALVES = [(0, 512), (512, 512)]
 WEIGHT_PIECES = [(0, 128), (128, 128), (256, 256), (512, 256), (768, 256)]
 PIECES = {0: [(0, 128), (128, 384), (512, 512)], 3: HALVES, 5: HALVES}
@@ -50,8 +51,7 @@ def tile_list_heads_tm_silu_kernel(tc, xT, w_words, w_scales, wgt, b, offs, out)
         planes = [keep.tile([P, T], F32, name=f"plane{u}", tag=f"plane{u}", align_bytes=64) for u in range(PLANES)]
         offsets = keep.tile([P, S // LANES], U16, name="offsets")
         w_codes = keep.tile([P, PASSES, M], U32, name="w_codes", align_bytes=64)
-        shared_planes = keep.tile([P, 512], U8, name="shared_planes", align_bytes=64)
-        w_scale_rows = shared_planes[:, 0 : PASSES * M].rearrange("p (a n) -> p a n", a=PASSES)
+        w_scale_rows = keep.tile([P, PASSES, M], U8, name="w_scale_rows", align_bytes=64)
 
         b_row = keep.tile([P, P], F32, name="b_row")
         nc.vector.memset(b_row[:], 0.0)
@@ -67,7 +67,7 @@ def tile_list_heads_tm_silu_kernel(tc, xT, w_words, w_scales, wgt, b, offs, out)
         warm_up = keep.tile([P, 1], F32, name="warm_up")
         nc.vector.memset(warm_up[:], 0.0)
         nc.scalar.activation(warm_up[:], warm_up[:], SILU)
-        nc.vector.memset(shared_planes[:].bitcast(I32), 0)
+        nc.vector.memset(w_scale_rows[:].rearrange("p a n -> p (a n)").bitcast(I32), 0)
 
         nc.sync.dma_start(w_codes[:].bitcast(I32), w_words.rearrange("a p n i -> p a (n i)").bitcast(I32))
         scale_source = w_scales.bitcast(I32).rearrange("a q n -> q a n")
@@ -95,13 +95,12 @@ def tile_list_heads_tm_silu_kernel(tc, xT, w_words, w_scales, wgt, b, offs, out)
                     identity[:],
                 )
             nc.scalar.copy(token_weights[:, j0 : j0 + n], turned_back[:])
-        first_weights = keep.tile([P, 512], F32, name="first_weights", tag="spread4", align_bytes=64)
-        nc.scalar.copy(first_weights[:], token_weights[:, 0:512])
+        first_weights = keep.tile([P, SLICE], F32, name="first_weights", tag="spread4", align_bytes=64)
+        nc.scalar.copy(first_weights[:], token_weights[:, 0:SLICE])
 
         grouped = [keep.tile([P, S, PACK], BF16, name=f"grouped{a}", align_bytes=64) for a in range(PASSES)]
         scales = [keep.tile([P, S], U8, name=f"scales{a}", align_bytes=64) for a in range(PASSES)]
-        codes = [keep.tile([P, S], U32, name=f"codes{a}", align_bytes=64) for a in range(PASSES)]
-        apart = {}
+        codes = {1: keep.tile([P, S], U32, name="codes1", align_bytes=64)}
 
         def gather(picked, u, j0, n, weights=None):
             nc.vector.tensor_tensor(
@@ -111,84 +110,40 @@ def tile_list_heads_tm_silu_kernel(tc, xT, w_words, w_scales, wgt, b, offs, out)
                 MULT,
             )
 
-        def interleave(copy, picked, u, j0, n):
+        def interleave(picked, u, j0, n):
             i0 = u % PACK
-            copy(
+            nc.scalar.copy(
                 grouped[u // PACK][:, j0 : j0 + n, i0 : i0 + 2].rearrange("p (s c t) i -> p s c t i", c=2, t=P),
                 picked.rearrange("p i (s t c) -> p s c t i", c=2, t=P),
             )
 
-        def interleave_half(copy, picked, u, j0, c):
-            i0 = u % PACK
-            copy(
-                grouped[u // PACK][:, j0 + c * P : j0 + (c + 1) * P, i0 : i0 + 2],
-                picked.rearrange("p i (t c) -> p c t i", c=2)[:, c],
-            )
-
-        def codes_of(a, j0, n):
-            for (pass_apart, begin), tile_apart in apart.items():
-                if pass_apart == a and j0 >= begin:
-                    return tile_apart[:, j0 - begin : j0 - begin + n].bitcast(FP8X4)
-            return codes[a][:, j0 : j0 + n].bitcast(FP8X4)
-
-        def scales_of(a, j0, n):
-            if a == 0 and j0 >= 512:
-                return shared_planes[4:P, j0 - 512 : j0 - 512 + n]
-            return scales[a][:, j0 : j0 + n]
-
-        def quantise(a, j0, n):
+        def quantise(a, s):
+            j0 = s * SLICE
             nc.vector.quantize_mx(
-                out=codes_of(a, j0, n),
-                scales=scales_of(a, j0, n),
-                in_=grouped[a][:, j0 : j0 + n, :].rearrange("p j i -> p (j i)"),
+                out=codes[a][:, j0 : j0 + SLICE].bitcast(FP8X4),
+                scales=scales[a][:, j0 : j0 + SLICE],
+                in_=grouped[a][:, j0 : j0 + SLICE, :].rearrange("p j i -> p (j i)"),
             )
+            for c in range(SLICE // P):
+                first = j0 + c * P
+                nc.tensor.matmul_mx(
+                    out=sums[s][:, c, :],
+                    lhsT=codes[a][:, first : first + P].bitcast(FP8X4),
+                    lhsT_scale=scales[a][:, first : first + P],
+                    rhs=w_codes[:, a, :].bitcast(FP8X4),
+                    rhs_scale=w_scale_rows[:, a, :],
+                    start=(a == 0 and c == 0),
+                    stop=(a == PASSES - 1 and c == SLICE // P - 1),
+                )
 
-        def pass_turned(acc, a, j0, n):
-            nc.tensor.matmul_mx(
-                out=acc[:],
-                lhsT=w_codes[:, a, :].bitcast(FP8X4),
-                lhsT_scale=w_scale_rows[:, a, :],
-                rhs=codes_of(a, j0, n),
-                rhs_scale=scales_of(a, j0, n),
-                start=(a == 0),
-                stop=(a == PASSES - 1),
-            )
-
-        def silu_turned(acc, j0, n):
-            columns = keep.tile([P, n], F32, name=f"columns{j0}")
-            nc.scalar.activation(columns[:], acc[:], SILU, bias=b_column[:])
-            return columns
-
-        def turn(columns, index, j0, n):
-            turned = bank(index, [P, n // P, P], f"turned{j0}")
-            for c in range(n // P):
-                nc.tensor.transpose(turned[:, c, :], columns[:, c * P : (c + 1) * P], identity[:])
-            return turned
-
-        def store_turned(turned, j0, n):
-            rows = keep.tile([P, n // P, P], F32, name=f"rows{j0}")
-            nc.scalar.copy(rows[:], turned[:])
-            nc.sync.dma_start(out[j0 : j0 + n, :].rearrange("(p c) n -> p c n", p=P), rows[:])
-
-        def pass_direct(acc, a, j0, c, blocks):
-            first = j0 + c * P
-            nc.tensor.matmul_mx(
-                out=acc[:, c, :],
-                lhsT=codes_of(a, first, P),
-                lhsT_scale=scales_of(a, first, P),
-                rhs=w_codes[:, a, :].bitcast(FP8X4),
-                rhs_scale=w_scale_rows[:, a, :],
-                start=(a == 0 and c == 0),
-                stop=(a == PASSES - 1 and c == blocks - 1),
-            )
-
-        def add_bias(biased, acc, n):
-            nc.vector.tensor_tensor(biased, acc[:], b_rows[:].unsqueeze(1).to_broadcast([P, n // P, P]), ADD)
-
-        def store_direct(store, biased, j0, n):
-            rows = keep.tile([P, n // P, P], F32, name=f"rows{j0}")
-            nc.scalar.activation(rows[:], biased, SILU)
-            store(out[j0 : j0 + n, :].rearrange("(p c) n -> p c n", p=P), rows[:])
+        def finish(s):
+            j0 = s * SLICE
+            biased = keep.tile([P, SLICE // P, M], F32, name=f"biased{s}")
+            nc.vector.tensor_tensor(biased[:], sums[s][:], b_rows[:].unsqueeze(1).to_broadcast([P, SLICE // P, M]), ADD)
+            rows = keep.tile([P, SLICE // P, M], F32, name=f"rows{s}")
+            nc.scalar.activation(rows[:], biased[:], SILU)
+            store = nc.scalar.dma_start if s == SLICES - 1 else nc.sync.dma_start
+            store(out[j0 : j0 + SLICE, :].rearrange("(p c) n -> p c n", p=P), rows[:])
 
         for u0 in (0, 2, 4):
             picked = keep.tile([P, 2, S], F32, name=f"picked{u0}", tag=f"picked{u0}", align_bytes=64)
@@ -196,7 +151,7 @@ def tile_list_heads_tm_silu_kernel(tc, xT, w_words, w_scales, wgt, b, offs, out)
                 for j0, n in PIECES.get(u, [(0, S)]):
                     gather(picked[:, u - u0, j0 : j0 + n], u, j0, n)
             for j0, n in HALVES if u0 > 0 else [(0, S)]:
-                interleave(nc.scalar.copy, picked[:, :, j0 : j0 + n], u0, j0, n)
+                interleave(picked[:, :, j0 : j0 + n], u0, j0, n)
 
         b_upright = bank(4, [P, P], "b_upright")
         nc.tensor.transpose(b_upright[:], b_row[:], identity[:])
@@ -207,52 +162,23 @@ def tile_list_heads_tm_silu_kernel(tc, xT, w_words, w_scales, wgt, b, offs, out)
         b_rows = keep.tile([P, P], F32, name="b_rows")
         nc.scalar.copy(b_rows[:], b_turned[:])
 
-        quantise(0, 0, 512)
-        late = keep.tile([P, 2, 768], F32, name="late")
-        gather(late[:, 0, :], 6, 0, 768)
-        for j0 in (0, 256, 512):
-            gather(late[:, 1, j0 : j0 + 256], 7, j0, 256, first_weights[:, j0 : j0 + 256] if j0 < 512 else None)
-        apart[0, 512] = keep.tile([P, 512], U32, name="codes_late", tag="spread4", align_bytes=64)
-        quantise(0, 512, 512)
-        for j0 in (0, 256, 512):
-            interleave(nc.scalar.copy, late[:, :, j0 : j0 + 256], 6, j0, 256)
-        acc_a = bank(0, [P, 256], "acc_a")
-        acc_b = bank(1, [P, 256], "acc_b")
-        acc_c = bank(6, [P, 2, P], "acc_c")
-        acc_d = bank(5, [P, 1, P], "acc_d")
-        acc_e = bank(7, [P, 1, P], "acc_e")
-        pass_turned(acc_a, 0, 0, 256)
-        pass_direct(acc_c, 0, 512, 0, 2)
-        pass_direct(acc_c, 0, 512, 1, 2)
-        pass_direct(acc_d, 0, 768, 0, 1)
-        back = late[:, 0, 0:512].rearrange("p (i j) -> p i j", i=2)
-        quantise(1, 0, 256)
-        gather(back[:, 0, :], 6, 768, 256)
-        quantise(1, 256, 256)
-        gather(back[:, 1, :], 7, 768, 256)
-        quantise(1, 512, 256)
-        interleave_half(nc.vector.tensor_copy, back, 6, 768, 0)
-        interleave_half(nc.vector.tensor_copy, back, 6, 768, 1)
-        quantise(1, 768, P)
-        quantise(1, 896, P)
-        pass_turned(acc_a, 1, 0, 256)
-        pass_turned(acc_b, 0, 256, 256)
-        pass_direct(acc_e, 0, 896, 0, 1)
-        pass_turned(acc_b, 1, 256, 256)
-        columns_a = silu_turned(acc_a, 0, 256)
-        columns_b = silu_turned(acc_b, 256, 256)
-        turned_a = turn(columns_a, 2, 0, 256)
-        turned_b = turn(columns_b, 3, 256, 256)
-        for c in range(2):
-            pass_direct(acc_c, 1, 512, c, 2)
-        pass_direct(acc_d, 1, 768, 0, 1)
-        pass_direct(acc_e, 1, 896, 0, 1)
-        store_turned(turned_a, 0, 256)
-        store_turned(turned_b, 256, 256)
-        biased_c = grouped[1][:, 768:896, :].rearrange("p j i -> p (j i)").bitcast(F32).rearrange("p (c n) -> p c n", n=P)
-        biased_last = keep.tile([P, 2, P], F32, name="biased_last")
-        add_bias(biased_c, acc_c, 256)
-        add_bias(biased_last[:, 0:1, :], acc_d, P)
-        add_bias(biased_last[:, 1:2, :], acc_e, P)
-        store_direct(nc.sync.dma_start, biased_c, 512, 256)
-        store_direct(nc.scalar.dma_start, biased_last[:], 768, 256)
+        late = keep.tile([P, 2, S], F32, name="late")
+        gather(late[:, 0, :], 6, 0, S)
+        for s in range(SLICES):
+            j0 = s * SLICE
+            gather(late[:, 1, j0 : j0 + SLICE], 7, j0, SLICE, first_weights[:] if s == 0 else None)
+            interleave(late[:, :, j0 : j0 + SLICE], 6, j0, SLICE)
+        codes[0] = keep.tile([P, S], U32, name="codes0", tag="spread4", align_bytes=64)
+        sums = [bank(s, [P, SLICE // P, M], f"sums{s}") for s in range(SLICES)]
+        quantise(0, 0)
+        quantise(1, 0)
+        quantise(0, 1)
+        quantise(1, 1)
+        quantise(0, 2)
+        quantise(0, 3)
+        quantise(1, 2)
+        finish(0)
+        quantise(1, 3)
+        finish(1)
+        finish(2)
+        finish(3)

@@ -27,9 +27,10 @@ BLOCKS = S // P
 
 SLICE = 256
 SLICES = S // SLICE
+TURNED = 0
 HALVES = [(0, 512), (512, 512)]
 WEIGHT_PIECES = [(0, 128), (128, 128), (256, 256), (512, 256), (768, 256)]
-PIECES = {0: [(0, 128), (128, 384), (512, 512)], 3: HALVES, 5: HALVES}
+PIECES = {0: [(0, 128), (128, 384), (512, 512)], 5: HALVES}
 
 
 def tile_list_heads_tm_silu_kernel(tc, xT, w_words, w_scales, wgt, b, offs, out):
@@ -117,13 +118,29 @@ def tile_list_heads_tm_silu_kernel(tc, xT, w_words, w_scales, wgt, b, offs, out)
                 picked.rearrange("p i (s t c) -> p s c t i", c=2, t=P),
             )
 
-        def quantise(a, s):
-            j0 = s * SLICE
+        def quantise(a, first_slice, slices):
+            j0, n = first_slice * SLICE, slices * SLICE
             nc.vector.quantize_mx(
-                out=codes[a][:, j0 : j0 + SLICE].bitcast(FP8X4),
-                scales=scales[a][:, j0 : j0 + SLICE],
-                in_=grouped[a][:, j0 : j0 + SLICE, :].rearrange("p j i -> p (j i)"),
+                out=codes[a][:, j0 : j0 + n].bitcast(FP8X4),
+                scales=scales[a][:, j0 : j0 + n],
+                in_=grouped[a][:, j0 : j0 + n, :].rearrange("p j i -> p (j i)"),
             )
+            for s in range(first_slice, first_slice + slices):
+                multiply(a, s)
+
+        def multiply(a, s):
+            j0 = s * SLICE
+            if s < TURNED:
+                nc.tensor.matmul_mx(
+                    out=sums[s][:].rearrange("p c n -> p (c n)"),
+                    lhsT=w_codes[:, a, :].bitcast(FP8X4),
+                    lhsT_scale=w_scale_rows[:, a, :],
+                    rhs=codes[a][:, j0 : j0 + SLICE].bitcast(FP8X4),
+                    rhs_scale=scales[a][:, j0 : j0 + SLICE],
+                    start=(a == 0),
+                    stop=(a == PASSES - 1),
+                )
+                return
             for c in range(SLICE // P):
                 first = j0 + c * P
                 nc.tensor.matmul_mx(
@@ -138,10 +155,18 @@ def tile_list_heads_tm_silu_kernel(tc, xT, w_words, w_scales, wgt, b, offs, out)
 
         def finish(s):
             j0 = s * SLICE
-            biased = keep.tile([P, SLICE // P, M], F32, name=f"biased{s}")
-            nc.vector.tensor_tensor(biased[:], sums[s][:], b_rows[:].unsqueeze(1).to_broadcast([P, SLICE // P, M]), ADD)
             rows = keep.tile([P, SLICE // P, M], F32, name=f"rows{s}")
-            nc.scalar.activation(rows[:], biased[:], SILU)
+            if s < TURNED:
+                columns = keep.tile([P, SLICE // P, P], F32, name=f"columns{s}")
+                nc.scalar.activation(columns[:], sums[s][:], SILU, bias=b_column[:])
+                turned = bank(SLICES + s, [P, SLICE // P, M], f"turned{s}")
+                for c in range(SLICE // P):
+                    nc.tensor.transpose(turned[:, c, :], columns[:, c, :], identity[:])
+                nc.scalar.copy(rows[:], turned[:])
+            else:
+                biased = keep.tile([P, SLICE // P, M], F32, name=f"biased{s}")
+                nc.vector.tensor_tensor(biased[:], sums[s][:], b_rows[:].unsqueeze(1).to_broadcast([P, SLICE // P, M]), ADD)
+                nc.scalar.activation(rows[:], biased[:], SILU)
             store = nc.scalar.dma_start if s == SLICES - 1 else nc.sync.dma_start
             store(out[j0 : j0 + SLICE, :].rearrange("(p c) n -> p c n", p=P), rows[:])
 
@@ -164,21 +189,20 @@ def tile_list_heads_tm_silu_kernel(tc, xT, w_words, w_scales, wgt, b, offs, out)
 
         late = keep.tile([P, 2, S], F32, name="late")
         gather(late[:, 0, :], 6, 0, S)
-        for s in range(SLICES):
-            j0 = s * SLICE
-            gather(late[:, 1, j0 : j0 + SLICE], 7, j0, SLICE, first_weights[:] if s == 0 else None)
-            interleave(late[:, :, j0 : j0 + SLICE], 6, j0, SLICE)
+        for j0, n in [(0, 256), (256, 256), (512, 512)]:
+            gather(late[:, 1, j0 : j0 + n], 7, j0, n, first_weights[:] if j0 == 0 else None)
+            for j in range(j0, j0 + n, SLICE):
+                interleave(late[:, :, j : j + SLICE], 6, j, SLICE)
         codes[0] = keep.tile([P, S], U32, name="codes0", tag="spread4", align_bytes=64)
         sums = [bank(s, [P, SLICE // P, M], f"sums{s}") for s in range(SLICES)]
-        quantise(0, 0)
-        quantise(1, 0)
-        quantise(0, 1)
-        quantise(1, 1)
-        quantise(0, 2)
-        quantise(0, 3)
-        quantise(1, 2)
+        quantise(0, 0, 1)
+        quantise(1, 0, 1)
+        quantise(0, 1, 1)
+        quantise(1, 1, 1)
+        quantise(0, 2, 2)
+        quantise(1, 2, 1)
+        quantise(1, 3, 1)
         finish(0)
-        quantise(1, 3)
         finish(1)
         finish(2)
         finish(3)

@@ -57,7 +57,9 @@ def tile_list_heads_tm_silu_kernel(tc, xT, w_words, w_scales, wgt, b, offs, out)
         b_row = keep.tile([P, P], F32, name="b_row")
         nc.vector.memset(b_row[:], 0.0)
         for u in range(PLANES):
-            nc.sync.dma_start(planes[u][:], plane_rows[u // PACK, u % PACK])
+            for parity in range(2 if u >= PACK else 1):
+                step = 2 if u >= PACK else 1
+                nc.sync.dma_start(planes[u][parity:P:step, :], plane_rows[u // PACK, u % PACK][parity:P:step, :])
             if u == 0:
                 nc.sync.dma_start(offsets[:], offs)
             if u == 1:
@@ -73,7 +75,7 @@ def tile_list_heads_tm_silu_kernel(tc, xT, w_words, w_scales, wgt, b, offs, out)
         nc.sync.dma_start(w_codes[:].bitcast(I32), w_words.rearrange("a p n i -> p a (n i)").bitcast(I32))
         scale_source = w_scales.bitcast(I32).rearrange("a q n -> q a n")
         for quadrant in range(4):
-            nc.gpsimd.dma_start(
+            nc.sync.dma_start(
                 w_scale_rows[32 * quadrant : 32 * quadrant + 4].bitcast(I32),
                 scale_source[4 * quadrant : 4 * quadrant + 4],
             )
@@ -201,8 +203,8 @@ def tile_list_heads_tm_silu_kernel(tc, xT, w_words, w_scales, wgt, b, offs, out)
         quantise(1, 1, 1)
         quantise(0, 2, 2)
         quantise(1, 2, 1)
-        quantise(1, 3, 1)
         finish(0)
+        quantise(1, 3, 1)
         finish(1)
         finish(2)
         finish(3)

@@ -56,7 +56,14 @@ def tile_list_heads_tm_silu_kernel(tc, xT, w_words, w_scales, wgt, b, offs, out)
 
         b_row = keep.tile([P, P], F32, name="b_row")
         nc.vector.memset(b_row[:], 0.0)
+        nc.vector.memset(w_scale_rows[:].rearrange("p a n -> p (a n)").bitcast(I32), 0)
+        scale_source = w_scales.bitcast(I32).rearrange("a q n -> q a n")
         for u in range(PLANES):
+            for quadrant in range(4 if u == PLANES - 1 else 0):
+                nc.sync.dma_start(
+                    w_scale_rows[32 * quadrant : 32 * quadrant + 4].bitcast(I32),
+                    scale_source[4 * quadrant : 4 * quadrant + 4],
+                )
             for parity in range(2 if u >= PACK else 1):
                 step = 2 if u >= PACK else 1
                 nc.sync.dma_start(planes[u][parity:P:step, :], plane_rows[u // PACK, u % PACK][parity:P:step, :])
@@ -70,15 +77,8 @@ def tile_list_heads_tm_silu_kernel(tc, xT, w_words, w_scales, wgt, b, offs, out)
         warm_up = keep.tile([P, 1], F32, name="warm_up")
         nc.vector.memset(warm_up[:], 0.0)
         nc.scalar.activation(warm_up[:], warm_up[:], SILU)
-        nc.vector.memset(w_scale_rows[:].rearrange("p a n -> p (a n)").bitcast(I32), 0)
 
         nc.sync.dma_start(w_codes[:].bitcast(I32), w_words.rearrange("a p n i -> p a (n i)").bitcast(I32))
-        scale_source = w_scales.bitcast(I32).rearrange("a q n -> q a n")
-        for quadrant in range(4):
-            nc.sync.dma_start(
-                w_scale_rows[32 * quadrant : 32 * quadrant + 4].bitcast(I32),
-                scale_source[4 * quadrant : 4 * quadrant + 4],
-            )
 
         small_columns = bank(7, [P, P], "small_columns")
         nc.tensor.transpose(small_columns[:], small_rows[:], identity[:])

@@ -30,7 +30,7 @@ SLICES = S // SLICE
 TURNED = 0
 HALVES = [(0, 512), (512, 512)]
 WEIGHT_PIECES = [(0, 128), (128, 128), (256, 256), (512, 256), (768, 256)]
-PIECES = {0: [(0, 128), (128, 384), (512, 512)], 5: HALVES}
+PIECES = {0: [(0, 128), (128, 384), (512, 512)], 3: HALVES, 5: HALVES}
 
 
 def tile_list_heads_tm_silu_kernel(tc, xT, w_words, w_scales, wgt, b, offs, out):
@@ -172,17 +172,25 @@ def tile_list_heads_tm_silu_kernel(tc, xT, w_words, w_scales, wgt, b, offs, out)
             store = nc.scalar.dma_start if s == SLICES - 1 else nc.sync.dma_start
             store(out[j0 : j0 + SLICE, :].rearrange("(p c) n -> p c n", p=P), rows[:])
 
-        for u0 in (0, 2, 4):
-            picked = keep.tile([P, 2, S], F32, name=f"picked{u0}", tag=f"picked{u0}", align_bytes=64)
-            for u in (u0, u0 + 1):
-                for j0, n in PIECES.get(u, [(0, S)]):
-                    gather(picked[:, u - u0, j0 : j0 + n], u, j0, n)
-            for j0, n in HALVES if u0 > 0 else [(0, S)]:
-                interleave(picked[:, :, j0 : j0 + n], u0, j0, n)
+        picked = keep.tile([P, PACK, S], F32, name="picked0", tag="picked0", align_bytes=64)
+        for u in range(PACK):
+            for j0, n in PIECES.get(u, [(0, S)]):
+                gather(picked[:, u, j0 : j0 + n], u, j0, n)
+        for j0 in range(0, S, SLICE):
+            nc.scalar.copy(
+                grouped[0][:, j0 : j0 + SLICE, :].rearrange("p (c t f) i -> p t i f c", c=2, f=2),
+                picked[:, :, j0 : j0 + SLICE].rearrange("p i (t f c) -> p t i f c", f=2, c=2),
+            )
+        picked = keep.tile([P, 2, S], F32, name="picked4", tag="picked4", align_bytes=64)
+        for u in (4, 5):
+            for j0, n in PIECES.get(u, [(0, S)]):
+                gather(picked[:, u - 4, j0 : j0 + n], u, j0, n)
+        for j0, n in HALVES:
+            interleave(picked[:, :, j0 : j0 + n], 4, j0, n)
 
         b_upright = bank(4, [P, P], "b_upright")
         nc.tensor.transpose(b_upright[:], b_row[:], identity[:])
-        b_column = keep.tile([P, 1], F32, name="b_column", tag="picked0", align_bytes=64)
+        b_column = keep.tile([P, 1], F32, name="b_column")
         nc.scalar.copy(b_column[:], b_upright[:, 0:1])
         b_turned = bank(4, [P, P], "b_turned")
         nc.tensor.transpose(b_turned[:], b_column[:].to_broadcast([P, P]), identity[:])

@@ -29,8 +29,9 @@ SLICE = 256
 SLICES = S // SLICE
 TURNED = 0
 HALVES = [(0, 512), (512, 512)]
-WEIGHT_PIECES = [(0, 128), (128, 128), (256, 256), (512, 256), (768, 256)]
-PIECES = {0: [(0, 128), (128, 384), (512, 512)], 3: HALVES, 5: HALVES}
+RUN = S // LANES
+SQUARE = 32
+PIECES = {3: HALVES, 5: HALVES}
 
 
 def tile_list_heads_tm_silu_kernel(tc, xT, w_words, w_scales, wgt, b, offs, out):
@@ -42,11 +43,10 @@ def tile_list_heads_tm_silu_kernel(tc, xT, w_words, w_scales, wgt, b, offs, out)
         def bank(index, shape, name):
             return psum.tile(shape, F32, name=name, tag=f"bank{index}")
 
-        small_rows = keep.tile([P, P], F32, name="small_rows")
-        nc.vector.memset(small_rows[64:128, :], 0.0)
+        runs = keep.tile([P, RUN], F32, name="runs", align_bytes=64)
         stride = 7 * S + S // 2
         halves = wgt.rearrange("r j -> (r j)")[7 * S : 7 * S + 16 * stride].rearrange("(q j) -> q j", q=16)
-        nc.sync.dma_start(small_rows[0:64, :], halves[:, 0 : S // 2].rearrange("q (h j) -> q h j", j=P))
+        nc.sync.dma_start(runs[:], halves[:, 0 : S // 2].rearrange("q (h j) -> q h j", j=RUN))
 
         plane_rows = xT.rearrange("(a p i) t -> a i p t", p=P, i=PACK)
         planes = [keep.tile([P, T], F32, name=f"plane{u}", tag=f"plane{u}", align_bytes=64) for u in range(PLANES)]
@@ -80,24 +80,19 @@ def tile_list_heads_tm_silu_kernel(tc, xT, w_words, w_scales, wgt, b, offs, out)
 
         nc.sync.dma_start(w_codes[:].bitcast(I32), w_words.rearrange("a p n i -> p a (n i)").bitcast(I32))
 
-        small_columns = bank(7, [P, P], "small_columns")
-        nc.tensor.transpose(small_columns[:], small_rows[:], identity[:])
-        token_weights = keep.tile([P, S], F32, name="token_weights")
-        for q, (j0, n) in enumerate(WEIGHT_PIECES):
-            spread = keep.tile([P, n // P, GROUPS, LANES], F32, name=f"spread{q}", tag=f"spread{q}", align_bytes=64)
-            by_block = small_columns[:, 0 : GROUPS * BLOCKS].rearrange("p (g k) -> p k g", g=GROUPS)
-            nc.vector.tensor_copy(
-                spread[:],
-                by_block[:, j0 // P : (j0 + n) // P, :].unsqueeze(3).to_broadcast([P, n // P, GROUPS, LANES]),
-            )
-            turned_back = bank(q, [P, n], f"turned_back{q}")
-            for c in range(n // P):
-                nc.tensor.transpose(
-                    turned_back[:, c * P : (c + 1) * P],
-                    spread[:, c].rearrange("p g l -> p (g l)"),
-                    identity[:],
-                )
-            nc.scalar.copy(token_weights[:, j0 : j0 + n], turned_back[:])
+        upright = keep.tile([P, RUN], F32, name="upright", align_bytes=64)
+        for c0 in range(0, RUN, SQUARE):
+            nc.vector.transpose(upright[:, c0 : c0 + SQUARE], runs[:, c0 : c0 + SQUARE])
+        by_run = upright[:].rearrange("p (m r) -> p r m", r=LANES)
+        token_weights = keep.tile([P, S], F32, name="token_weights", align_bytes=64)
+        for q in range(SLICES):
+            spread = keep.tile([P, 4, 4, LANES], F32, name=f"spread{q}", tag=f"spread{q}", align_bytes=64)
+            source = by_run[:, 4 * q : 4 * q + 4, :].unsqueeze(3).to_broadcast([P, 4, 4, LANES])
+            if q == 0:
+                nc.vector.tensor_copy(spread[:], source)
+            else:
+                nc.scalar.copy(spread[:], source)
+            nc.vector.transpose(token_weights[:, q * SLICE : (q + 1) * SLICE], spread[:].rearrange("p r m l -> p (r m l)"))
         first_weights = keep.tile([P, SLICE], F32, name="first_weights", tag="spread4", align_bytes=64)
         nc.scalar.copy(first_weights[:], token_weights[:, 0:SLICE])
 

@@ -115,6 +115,16 @@ def tile_list_heads_tm_silu_kernel(tc, xT, w_words, w_scales, wgt, b, offs, out)
                 picked.rearrange("p i (s t c) -> p s c t i", c=2, t=P),
             )
 
+        def quantise_by_blocks(a, s):
+            for c in range(SLICE // P):
+                first = s * SLICE + c * P
+                nc.vector.quantize_mx(
+                    out=codes[a][:, first : first + P].bitcast(FP8X4),
+                    scales=scales[a][:, first : first + P],
+                    in_=grouped[a][:, first : first + P, :].rearrange("p j i -> p (j i)"),
+                )
+            multiply(a, s)
+
         def quantise(a, first_slice, slices):
             j0, n = first_slice * SLICE, slices * SLICE
             nc.vector.quantize_mx(
@@ -207,7 +217,7 @@ def tile_list_heads_tm_silu_kernel(tc, xT, w_words, w_scales, wgt, b, offs, out)
         quantise(0, 2, 2)
         quantise(1, 2, 1)
         finish(0)
-        quantise(1, 3, 1)
+        quantise_by_blocks(1, 3)
         finish(1)
         finish(2)
         finish(3)

from contextlib import ExitStack

import concourse.mybir as mybir
from concourse.masks import make_identity

F32 = mybir.dt.float32
BF16 = mybir.dt.bfloat16
I32 = mybir.dt.int32
U32 = mybir.dt.uint32
U16 = mybir.dt.uint16
U8 = mybir.dt.uint8
FP8X4 = mybir.dt.float8_e4m3fn_x4
MULT = mybir.AluOpType.mult
ADD = mybir.AluOpType.add
SILU = mybir.ActivationFunctionType.Silu

K, M, T, S = 1024, 128, 2048, 1024
FLOPS = 2 * K * M * S

P = 128
PACK = 4
PASSES = K // (P * PACK)
PLANES = PASSES * PACK
LANES = 16
GROUPS = P // LANES
BLOCKS = S // P

SLICE = 256
SLICES = S // SLICE
TURNED = 0
HALVES = [(0, 512), (512, 512)]
RUN = S // LANES
SQUARE = 32
PIECES = {3: HALVES, 5: HALVES}


def tile_list_heads_tm_silu_kernel(tc, xT, w_words, w_scales, wgt, b, offs, out):
    nc = tc.nc
    with ExitStack() as ctx:
        keep = ctx.enter_context(tc.tile_pool(name="keep", bufs=1))
        psum = ctx.enter_context(tc.psum_pool(name="psum", bufs=1))

        def bank(index, shape, name):
            return psum.tile(shape, F32, name=name, tag=f"bank{index}")

        runs = keep.tile([P, RUN], F32, name="runs", align_bytes=64)
        stride = 7 * S + S // 2
        halves = wgt.rearrange("r j -> (r j)")[7 * S : 7 * S + 16 * stride].rearrange("(q j) -> q j", q=16)
        nc.sync.dma_start(runs[:], halves[:, 0 : S // 2].rearrange("q (h j) -> q h j", j=RUN))

        plane_rows = xT.rearrange("(a p i) t -> a i p t", p=P, i=PACK)
        planes = [keep.tile([P, T], F32, name=f"plane{u}", tag=f"plane{u}", align_bytes=64) for u in range(PLANES)]
        offsets = keep.tile([P, S // LANES], U16, name="offsets")
        w_codes = keep.tile([P, PASSES, M], U32, name="w_codes", align_bytes=64)
        w_scale_rows = keep.tile([P, PASSES, M], U8, name="w_scale_rows", align_bytes=64)

        b_row = keep.tile([P, P], F32, name="b_row")
        nc.vector.memset(b_row[:], 0.0)
        nc.vector.memset(w_scale_rows[:].rearrange("p a n -> p (a n)").bitcast(I32), 0)
        scale_source = w_scales.bitcast(I32).rearrange("a q n -> q a n")
        for u in range(PLANES):
            for quadrant in range(4 if u == PLANES - 1 else 0):
                nc.sync.dma_start(
                    w_scale_rows[32 * quadrant : 32 * quadrant + 4].bitcast(I32),
                    scale_source[4 * quadrant : 4 * quadrant + 4],
                )
            for parity in range(2 if u >= PACK else 1):
                step = 2 if u >= PACK else 1
                nc.sync.dma_start(planes[u][parity:P:step, :], plane_rows[u // PACK, u % PACK][parity:P:step, :])
            if u == 0:
                nc.sync.dma_start(offsets[:], offs)
            if u == 1:
                nc.sync.dma_start(b_row[0:1, :], b.rearrange("(o n) -> o n", o=1))

        identity = keep.tile([P, P], F32, name="identity")
        make_identity(nc, identity[:])
        warm_up = keep.tile([P, 1], F32, name="warm_up")
        nc.vector.memset(warm_up[:], 0.0)
        nc.scalar.activation(warm_up[:], warm_up[:], SILU)

        nc.sync.dma_start(w_codes[:].bitcast(I32), w_words.rearrange("a p n i -> p a (n i)").bitcast(I32))

        upright = keep.tile([P, RUN], F32, name="upright", align_bytes=64)
        for c0 in range(0, RUN, SQUARE):
            nc.vector.transpose(upright[:, c0 : c0 + SQUARE], runs[:, c0 : c0 + SQUARE])
        by_run = upright[:].rearrange("p (m r) -> p r m", r=LANES)
        token_weights = keep.tile([P, S], F32, name="token_weights", align_bytes=64)
        for q in range(SLICES):
            spread = keep.tile([P, 4, 4, LANES], F32, name=f"spread{q}", tag=f"spread{q}", align_bytes=64)
            source = by_run[:, 4 * q : 4 * q + 4, :].unsqueeze(3).to_broadcast([P, 4, 4, LANES])
            if q == 0:
                nc.vector.tensor_copy(spread[:], source)
            else:
                nc.scalar.copy(spread[:], source)
            nc.vector.transpose(token_weights[:, q * SLICE : (q + 1) * SLICE], spread[:].rearrange("p r m l -> p (r m l)"))
        first_weights = keep.tile([P, SLICE], F32, name="first_weights", tag="spread4", align_bytes=64)
        nc.scalar.copy(first_weights[:], token_weights[:, 0:SLICE])

        grouped = [keep.tile([P, S, PACK], BF16, name=f"grouped{a}", align_bytes=64) for a in range(PASSES)]
        scales = [keep.tile([P, S], U8, name=f"scales{a}", align_bytes=64) for a in range(PASSES)]
        codes = {1: keep.tile([P, S], U32, name="codes1", align_bytes=64)}

        def gather(picked, u, j0, n, weights=None):
            nc.vector.tensor_tensor(
                picked,
                planes[u][:].indirect(offsets[:, j0 // LANES : (j0 + n) // LANES]),
                token_weights[:, j0 : j0 + n] if weights is None else weights,
                MULT,
            )

        def interleave(picked, u, j0, n):
            i0 = u % PACK
            nc.scalar.copy(
                grouped[u // PACK][:, j0 : j0 + n, i0 : i0 + 2].rearrange("p (s c t) i -> p s c t i", c=2, t=P),
                picked.rearrange("p i (s t c) -> p s c t i", c=2, t=P),
            )

        def quantise_by_blocks(a, s):
            for c in range(SLICE // P):
                first = s * SLICE + c * P
                nc.vector.quantize_mx(
                    out=codes[a][:, first : first + P].bitcast(FP8X4),
                    scales=scales[a][:, first : first + P],
                    in_=grouped[a][:, first : first + P, :].rearrange("p j i -> p (j i)"),
                )
            multiply(a, s)

        def quantise(a, first_slice, slices):
            j0, n = first_slice * SLICE, slices * SLICE
            nc.vector.quantize_mx(
                out=codes[a][:, j0 : j0 + n].bitcast(FP8X4),
                scales=scales[a][:, j0 : j0 + n],
                in_=grouped[a][:, j0 : j0 + n, :].rearrange("p j i -> p (j i)"),
            )
            for s in range(first_slice, first_slice + slices):
                multiply(a, s)

        def multiply(a, s):
            j0 = s * SLICE
            if s < TURNED:
                nc.tensor.matmul_mx(
                    out=sums[s][:].rearrange("p c n -> p (c n)"),
                    lhsT=w_codes[:, a, :].bitcast(FP8X4),
                    lhsT_scale=w_scale_rows[:, a, :],
                    rhs=codes[a][:, j0 : j0 + SLICE].bitcast(FP8X4),
                    rhs_scale=scales[a][:, j0 : j0 + SLICE],
                    start=(a == 0),
                    stop=(a == PASSES - 1),
                )
                return
            for c in range(SLICE // P):
                first = j0 + c * P
                nc.tensor.matmul_mx(
                    out=sums[s][:, c, :],
                    lhsT=codes[a][:, first : first + P].bitcast(FP8X4),
                    lhsT_scale=scales[a][:, first : first + P],
                    rhs=w_codes[:, a, :].bitcast(FP8X4),
                    rhs_scale=w_scale_rows[:, a, :],
                    start=(a == 0 and c == 0),
                    stop=(a == PASSES - 1 and c == SLICE // P - 1),
                )

        def finish(s):
            j0 = s * SLICE
            rows = keep.tile([P, SLICE // P, M], F32, name=f"rows{s}")
            if s < TURNED:
                columns = keep.tile([P, SLICE // P, P], F32, name=f"columns{s}")
                nc.scalar.activation(columns[:], sums[s][:], SILU, bias=b_column[:])
                turned = bank(SLICES + s, [P, SLICE // P, M], f"turned{s}")
                for c in range(SLICE // P):
                    nc.tensor.transpose(turned[:, c, :], columns[:, c, :], identity[:])
                nc.scalar.copy(rows[:], turned[:])
            else:
                biased = keep.tile([P, SLICE // P, M], F32, name=f"biased{s}")
                nc.vector.tensor_tensor(biased[:], sums[s][:], b_rows[:].unsqueeze(1).to_broadcast([P, SLICE // P, M]), ADD)
                nc.scalar.activation(rows[:], biased[:], SILU)
            store = nc.scalar.dma_start if s == SLICES - 1 else nc.sync.dma_start
            store(out[j0 : j0 + SLICE, :].rearrange("(p c) n -> p c n", p=P), rows[:])

        picked = keep.tile([P, PACK, S], F32, name="picked0", tag="picked0", align_bytes=64)
        for u in range(PACK):
            for j0, n in PIECES.get(u, [(0, S)]):
                gather(picked[:, u, j0 : j0 + n], u, j0, n)
        for j0 in range(0, S, SLICE):
            nc.scalar.copy(
                grouped[0][:, j0 : j0 + SLICE, :].rearrange("p (c t f) i -> p t i f c", c=2, f=2),
                picked[:, :, j0 : j0 + SLICE].rearrange("p i (t f c) -> p t i f c", f=2, c=2),
            )
        picked = keep.tile([P, 2, S], F32, name="picked4", tag="picked4", align_bytes=64)
        for u in (4, 5):
            for j0, n in PIECES.get(u, [(0, S)]):
                gather(picked[:, u - 4, j0 : j0 + n], u, j0, n)
        for j0, n in HALVES:
            interleave(picked[:, :, j0 : j0 + n], 4, j0, n)

        b_upright = bank(4, [P, P], "b_upright")
        nc.tensor.transpose(b_upright[:], b_row[:], identity[:])
        b_column = keep.tile([P, 1], F32, name="b_column")
        nc.scalar.copy(b_column[:], b_upright[:, 0:1])
        b_turned = bank(4, [P, P], "b_turned")
        nc.tensor.transpose(b_turned[:], b_column[:].to_broadcast([P, P]), identity[:])
        b_rows = keep.tile([P, P], F32, name="b_rows")
        nc.scalar.copy(b_rows[:], b_turned[:])

        late = keep.tile([P, 2, S], F32, name="late")
        gather(late[:, 0, :], 6, 0, S)
        for j0, n in [(0, 256), (256, 256), (512, 512)]:
            gather(late[:, 1, j0 : j0 + n], 7, j0, n, first_weights[:] if j0 == 0 else None)
            for j in range(j0, j0 + n, SLICE):
                interleave(late[:, :, j : j + SLICE], 6, j, SLICE)
        codes[0] = keep.tile([P, S], U32, name="codes0", tag="spread4", align_bytes=64)
        sums = [bank(s, [P, SLICE // P, M], f"sums{s}") for s in range(SLICES)]
        quantise(0, 0, 1)
        quantise(1, 0, 1)
        quantise(0, 1, 1)
        quantise(1, 1, 1)
        quantise(0, 2, 2)
        quantise(1, 2, 1)
        finish(0)
        quantise_by_blocks(1, 3)
        finish(1)
        finish(2)
        finish(3)
